import numpy as np
import ml_dtypes


def mxq(x, axis, fmt="e4m3"):
    dtype, down = {"e4m3": (ml_dtypes.float8_e4m3fn, 7), "e5m2": (ml_dtypes.float8_e5m2, 14)}[fmt]
    v = np.moveaxis(np.asarray(x, np.float32).astype(ml_dtypes.bfloat16).astype(np.float64), axis, -1)
    blocks = v.reshape(v.shape[:-1] + (-1, 32))
    amax = np.abs(blocks).max(-1, keepdims=True)
    byte = np.maximum(np.where(amax > 0, np.frexp(amax)[1] - 1 + 127, 0) - down, 1)
    scale = np.exp2(byte - 127.0)
    codes = (blocks / scale).astype(np.float32).astype(dtype).astype(np.float64)
    return np.moveaxis((codes * scale).reshape(v.shape), -1, axis)


WIDE = False


def mx_kscale(k):
    if not WIDE:
        return np.ones(k)
    levels = np.array([10, -10, 5, -5, 0])
    if k % 512:
        return np.exp2(np.random.permutation(np.resize(levels, k // 32))).repeat(32)
    a = np.empty((k // 512, 16))
    for p in range(k // 512):
        a[p, :8] = np.random.permutation(np.resize(levels, 8))
        for g in range(8):
            far = levels[np.abs(levels - a[p, g]) >= 10]
            a[p, g + 8] = far[np.random.randint(len(far))]
    return np.exp2(a.ravel()).repeat(32)


def f64(x):
    return np.asarray(x).astype(np.float64)


def striped(idx):
    return np.tile(idx.reshape(-1, 16).T, (8, 1)).astype(np.uint16)


def unstriped(offs):
    return offs[:16].T.reshape(-1).astype(np.int64)


def pack_weight(w):
    k, n = w.shape
    w = f64(np.asarray(w, np.float32).astype(ml_dtypes.bfloat16)).reshape(k // 32, 32, n)
    amax = np.abs(w).max(1)
    byte = np.clip(np.where(amax > 0, np.frexp(amax)[1] - 1 + 127 - 7, 1), 1, 254)
    scaled = (w * np.exp2(127.0 - byte)[:, None, :]).reshape(k, n).astype(np.float32)
    words = np.ascontiguousarray(scaled.reshape(k // 512, 128, 4, n).transpose(0, 1, 3, 2)).astype(ml_dtypes.float8_e4m3fn).view(np.uint8)
    return words, np.ascontiguousarray(byte.astype(np.uint8).reshape(k // 512, 16, n))


def unpack_weight(words, scales):
    g, p, n, _ = words.shape
    vals = np.ascontiguousarray(words).view(ml_dtypes.float8_e4m3fn).astype(np.float64) * np.repeat(np.exp2(scales.astype(np.float64) - 127.0), 8, axis=1)[..., None]
    return vals.transpose(0, 1, 3, 2).reshape(g * 512, n)


E2M1 = np.array([0.0, 0.5, 1.0, 1.5, 2.0, 3.0, 4.0, 6.0, -0.0, -0.5, -1.0, -1.5, -2.0, -3.0, -4.0, -6.0])


def pack_fp4(w):
    k, n = w.shape
    w = f64(np.asarray(w, np.float32).astype(ml_dtypes.bfloat16)).reshape(k // 32, 32, n)
    amax = np.abs(w).max(1)
    mant, ex = np.frexp(amax / 6.0)
    byte = np.clip(np.where(amax > 0, np.where(mant > 0.5, ex, ex - 1) + 127, 1), 1, 254)
    scaled = (w * np.exp2(127.0 - byte)[:, None, :]).reshape(k, n).astype(np.float32)
    c = np.ascontiguousarray(scaled.reshape(k // 512, 128, 4, n).transpose(0, 1, 3, 2)).astype(ml_dtypes.float4_e2m1fn).view(np.uint8) & 0xF
    words = (c[..., 0::2] | (c[..., 1::2] << 4)).reshape(k // 512, 128, 2 * n)
    return np.ascontiguousarray(words), np.ascontiguousarray(byte.astype(np.uint8).reshape(k // 512, 16, n))


def unpack_fp4(words, scales):
    g, _, n = scales.shape
    words = np.ascontiguousarray(words).reshape(g, 128, n, 2)
    nib = np.empty((g, 128, n, 4), np.uint8)
    nib[..., 0::2] = words & 0xF
    nib[..., 1::2] = words >> 4
    vals = E2M1[nib] * np.repeat(np.exp2(scales.astype(np.float64) - 127.0), 8, axis=1)[..., None]
    return vals.transpose(0, 1, 3, 2).reshape(g * 512, n)


def relu(v):
    return np.maximum(v, 0.0)


K, T, S, V, H, N = 512, 2048, 1024, 512, 512, 256


def setup_inputs():
    n = np.random.standard_normal
    s = mx_kscale(K)[:, None]
    u = mx_kscale(H)
    near = np.random.permutation(S)
    packed_xT = pack_weight(n((K, T)) * s)
    packed_w2 = pack_fp4(n((H, N)) / np.sqrt(2 * H) / u[:, None])
    packed_w3 = pack_fp4(n((H, N)) / np.sqrt(2 * H) / u[:, None])
    return {
        "x_words": packed_xT[0],
        "x_scales": packed_xT[1],
        "w1": (n((K, H)) / np.sqrt(K) / s * u).astype(np.float32),
        "w2_words": packed_w2[0],
        "w2_scales": packed_w2[1],
        "w3_words": packed_w3[0],
        "w3_scales": packed_w3[1],
        "offs": striped(np.random.permutation(T)[:S]),
        "pos1": striped(near[:V]),
        "pos2": striped(near[V:]),
        "foe1": striped(np.random.permutation(S)[:V]),
        "foe2": striped(np.random.permutation(S)[:V]),
    }


def reference(x_words, x_scales, w1, w2_words, w2_scales, w3_words, w3_scales, offs, pos1, pos2, foe1, foe2):
    xq = unpack_weight(x_words, x_scales)[:, unstriped(offs)]
    h = relu(mxq(f64(w1), 0, "e4m3").T @ xq)
    zp = np.maximum(h[:, unstriped(pos1)], h[:, unstriped(pos2)])
    zn = np.maximum(h[:, unstriped(foe1)], h[:, unstriped(foe2)])
    return np.tanh(unpack_fp4(w2_words, w2_scales).T @ mxq(zp, 0, "e4m3") + unpack_fp4(w3_words, w3_scales).T @ mxq(zn, 0, "e4m3"))

@@ -1,0 +1,212 @@
+from contextlib import ExitStack
+
+import concourse.mybir as mybir
+
+K, T, S, V, H, N = 512, 2048, 1024, 512, 512, 256
+FLOPS = 2 * K * H * S + 2 * 2 * H * N * V
+
+F32 = mybir.dt.float32
+BF16 = mybir.dt.bfloat16
+I32 = mybir.dt.int32
+U32 = mybir.dt.uint32
+U16 = mybir.dt.uint16
+U8 = mybir.dt.uint8
+FP8X4 = mybir.dt.float8_e4m3fn_x4
+FP4X4 = mybir.dt.float4_e2m1fn_x4
+MAX = mybir.AluOpType.max
+RELU = mybir.ActivationFunctionType.Relu
+TANH = mybir.ActivationFunctionType.Tanh
+
+P = 128
+PACK = 4
+CHUNK = 128
+CHUNKS = V // CHUNK
+BANK = 512
+
+
+def load_scale_rows(queue, plane, rows):
+    for q in range(4):
+        queue.dma_start(out=plane[32 * q : 32 * q + 4, :].bitcast(I32), in_=rows[4 * q : 4 * q + 4, :].bitcast(I32))
+
+
+def tile_picked_zsgn_max_p_kernel(
+    tc, x_words, x_scales, w1, w2_words, w2_scales, w3_words, w3_scales, offs, pos1, pos2, foe1, foe2, out
+):
+    nc = tc.nc
+    with ExitStack() as ctx:
+        lists = ctx.enter_context(tc.tile_pool(name="lists", bufs=1))
+        keep = ctx.enter_context(tc.tile_pool(name="keep", bufs=1))
+        psum = ctx.enter_context(tc.psum_pool(name="psum", bufs=1))
+
+        offs_sb = lists.tile([P, S // 16], U16, name="offs_sb")
+        pos1_sb = lists.tile([P, V // 16], U16, name="pos1_sb")
+        pos2_sb = lists.tile([P, V // 16], U16, name="pos2_sb")
+        foe1_sb = lists.tile([P, V // 16], U16, name="foe1_sb")
+        foe2_sb = lists.tile([P, V // 16], U16, name="foe2_sb")
+
+        x_scale_table = keep.tile([P, T], U8, name="x_scale_table", align_bytes=64)
+        nc.vector.memset(x_scale_table[:].bitcast(I32), 0)
+        zero = keep.tile([P, 1], F32, name="zero")
+        nc.vector.memset(zero[:], 0.0)
+        w23_scales = keep.tile([P, 2, N], U8, name="w23_scales", align_bytes=64)
+        nc.vector.memset(w23_scales[:].rearrange("p a n -> p (a n)").bitcast(I32), 0)
+
+        nc.sync.dma_start(offs_sb[:], offs)
+        w1_rows = w1.rearrange("(p j) c -> p j c", j=PACK)
+        w1_raw = [keep.tile([P, PACK, H // 2], F32, name="w1_raw%d" % u, align_bytes=64) for u in range(2)]
+        nc.sync.dma_start(out=w1_raw[0][:], in_=w1_rows[:, :, : H // 2])
+        nc.sync.dma_start(pos1_sb[:], pos1)
+        load_scale_rows(nc.sync, x_scale_table, x_scales[0])
+        nc.sync.dma_start(out=w1_raw[1][:], in_=w1_rows[:, :, H // 2 :])
+        x_word_table = keep.tile([P, T], I32, name="x_word_table", align_bytes=64)
+        nc.sync.dma_start(out=x_word_table[:], in_=x_words[0].rearrange("p n t -> p (n t)").bitcast(I32))
+        nc.sync.dma_start(pos2_sb[:], pos2)
+        nc.sync.dma_start(foe1_sb[:], foe1)
+        nc.sync.dma_start(foe2_sb[:], foe2)
+        w2_codes = keep.tile([P, 2 * N], U8, name="w2_codes", align_bytes=64)
+        w3_codes = keep.tile([P, 2 * N], U8, name="w3_codes", align_bytes=64)
+        nc.sync.dma_start(out=w2_codes[:].bitcast(I32), in_=w2_words[0].bitcast(I32))
+        nc.sync.dma_start(out=w3_codes[:].bitcast(I32), in_=w3_words[0].bitcast(I32))
+        load_scale_rows(nc.sync, w23_scales[:, 0, :], w2_scales[0])
+        load_scale_rows(nc.sync, w23_scales[:, 1, :], w3_scales[0])
+
+        relu_bias = keep.tile([P, 1], F32, name="relu_bias")
+        nc.scalar.activation(out=relu_bias[:], in_=zero[:], func=TANH)
+
+        x_sc = keep.tile([P, S], U8, name="x_sc", align_bytes=64)
+        nc.vector.tensor_copy(x_sc[:], x_scale_table[:].indirect(offs_sb[:]))
+
+        w1_bf = keep.tile([P, PACK, P, PACK], BF16, name="w1_bf", align_bytes=64)
+        dst = w1_bf[:].rearrange("p t m j -> p m j t")
+        for u in range(2):
+            nc.scalar.copy(
+                out=dst[:, u * P // 2 : (u + 1) * P // 2], in_=w1_raw[u][:].rearrange("p j (m t) -> p m j t", t=PACK)
+            )
+        w1_codes = keep.tile([P, H], U32, name="w1_codes", tag="late_a", align_bytes=64)
+        w1_sc = keep.tile([P, H], U8, name="w1_sc", align_bytes=64)
+        nc.vector.quantize_mx(
+            out=w1_codes[:].bitcast(FP8X4), scales=w1_sc[:], in_=w1_bf[:].rearrange("p t m j -> p (t m j)")
+        )
+
+        x_codes = keep.tile([P, S], U32, name="x_codes", align_bytes=64)
+        first_pieces = [(0, 512), (512, 768), (768, 1024)]
+        for a, b in first_pieces:
+            nc.vector.tensor_copy(
+                x_codes[:, a:b], x_word_table[:].bitcast(U32).indirect(offs_sb[:, a // 16 : b // 16])
+            )
+
+        h = [keep.tile([P, S], F32, name="h%d" % t, align_bytes=64) for t in range(PACK)]
+        bank = 0
+        for t in range(PACK):
+            pieces = first_pieces if t == 0 else [(0, 512), (512, 1024)]
+            for a, b in pieces:
+                acc = psum.tile([P, BANK], F32, name="acc%d" % bank, tag="bank%d" % (bank % 8))
+                bank += 1
+                nc.tensor.matmul_mx(
+                    out=acc[:, : b - a],
+                    lhsT=w1_codes[:, t * P : (t + 1) * P].bitcast(FP8X4),
+                    lhsT_scale=w1_sc[:, t * P : (t + 1) * P],
+                    rhs=x_codes[:, a:b].bitcast(FP8X4),
+                    rhs_scale=x_sc[:, a:b],
+                    start=True,
+                    stop=True,
+                )
+                if t == 0 and a == 0:
+                    nc.scalar.activation(out=h[t][:, a:b], in_=acc[:, : b - a], func=RELU, bias=relu_bias[:])
+                else:
+                    nc.scalar.activation(out=h[t][:, a:b], in_=acc[:, : b - a], func=RELU)
+
+        def fetch(dst_tile, t, list_sb, v0, v1):
+            nc.vector.tensor_copy(dst_tile[:, :, t, :], h[t][:].indirect(list_sb[:, v0 // 16 : v1 // 16]))
+
+        def larger(name, a, b, runs, run):
+            z = keep.tile([P, runs, PACK, run], BF16, name=name, align_bytes=64)
+            flat = "p r t v -> p (r t v)"
+            nc.vector.tensor_tensor(z[:].rearrange(flat), a[:].rearrange(flat), b[:].rearrange(flat), MAX)
+            return z
+
+        def weave(copy, woven, z, r, run):
+            copy(
+                out=woven[:, r * run : (r + 1) * run, :].rearrange("p (c i) t -> p c t i", i=4),
+                in_=z[:, r].rearrange("p t (c i) -> p c t i", i=4),
+            )
+
+        def quantise(codes, scales, woven, v0, v1, w0):
+            nc.vector.quantize_mx(
+                out=codes[:, v0:v1].bitcast(FP8X4),
+                scales=scales[:, v0:v1],
+                in_=woven[:, v0 - w0 : v1 - w0, :].rearrange("p v t -> p (v t)"),
+            )
+
+        accs = {}
+
+        def product(which, codes, scales, c):
+            w_codes = w2_codes if which == 0 else w3_codes
+            for b in range(N // P):
+                if which == 0:
+                    accs[(b, c)] = psum.tile([P, BANK], F32, name="out%d_%d" % (b, c), tag="bank%d" % ((1 + 2 * c + b) % 8))
+                nc.tensor.matmul_mx(
+                    out=accs[(b, c)][:, :CHUNK],
+                    lhsT=w_codes[:, 2 * P * b : 2 * P * (b + 1)].bitcast(FP4X4),
+                    lhsT_scale=w23_scales[:, which, P * b : P * (b + 1)],
+                    rhs=codes[:, c * CHUNK : (c + 1) * CHUNK].bitcast(FP8X4),
+                    rhs_scale=scales[:, c * CHUNK : (c + 1) * CHUNK],
+                    start=(which == 0),
+                    stop=(which == 1),
+                )
+
+        head = V - CHUNK
+        friend1 = keep.tile([P, CHUNKS, PACK, CHUNK], BF16, name="friend1", align_bytes=64)
+        friend2 = keep.tile([P, CHUNKS, PACK, CHUNK], BF16, name="friend2", tag="late_b", align_bytes=64)
+        for t in range(PACK):
+            fetch(friend1, t, pos1_sb, 0, V)
+            fetch(friend2, t, pos2_sb, 0, V)
+        foe1_head = keep.tile([P, CHUNKS - 1, PACK, CHUNK], BF16, name="foe1_head", tag="late_a", align_bytes=64)
+        fetch(foe1_head, 0, foe1_sb, 0, head)
+        zp = larger("zp", friend1, friend2, CHUNKS, CHUNK)
+        fetch(foe1_head, 1, foe1_sb, 0, head)
+        zp_woven = keep.tile([P, V, PACK], BF16, name="zp_woven", tag="late_c", align_bytes=64)
+        for c in range(CHUNKS):
+            weave(nc.scalar.copy, zp_woven, zp, c, CHUNK)
+        foe2_head = keep.tile([P, CHUNKS - 1, PACK, CHUNK], BF16, name="foe2_head", tag="late_b", align_bytes=64)
+        for t in range(PACK):
+            fetch(foe2_head, t, foe2_sb, 0, head)
+            if t >= 2:
+                fetch(foe1_head, t, foe1_sb, 0, head)
+        zn_head = larger("zn_head", foe1_head, foe2_head, CHUNKS - 1, CHUNK)
+        zp_codes = keep.tile([P, V], U32, name="zp_codes", align_bytes=64)
+        zp_sc = keep.tile([P, V], U8, name="zp_sc", align_bytes=64)
+        quantise(zp_codes, zp_sc, zp_woven, 0, V, 0)
+        for c in range(CHUNKS):
+            product(0, zp_codes, zp_sc, c)
+        zn_head_woven = keep.tile([P, head, PACK], BF16, name="zn_head_woven", align_bytes=64)
+        for c in range(CHUNKS - 1):
+            weave(nc.scalar.copy, zn_head_woven, zn_head, c, CHUNK)
+
+        foes_tail = keep.tile([P, 2, 2, PACK, CHUNK // 2], BF16, name="foes_tail", tag="late_c", align_bytes=64)
+        for t in range(PACK):
+            fetch(foes_tail[:, 0], t, foe1_sb, head, V)
+            fetch(foes_tail[:, 1], t, foe2_sb, head, V)
+        zn_codes = keep.tile([P, V], U32, name="zn_codes", align_bytes=64)
+        zn_sc = keep.tile([P, V], U8, name="zn_sc", align_bytes=64)
+        quantise(zn_codes, zn_sc, zn_head_woven, 0, 256, 0)
+        zn_tail = larger("zn_tail", foes_tail[:, 0], foes_tail[:, 1], 2, CHUNK // 2)
+        quantise(zn_codes, zn_sc, zn_head_woven, 256, head, 0)
+        zn_tail_woven = keep.tile([P, CHUNK, PACK], BF16, name="zn_tail_woven", align_bytes=64)
+        nc.vector.tensor_copy(
+            out=zn_tail_woven[:].rearrange("p (r c i) t -> p r c t i", r=2, i=4),
+            in_=zn_tail[:].rearrange("p r t (c i) -> p r c t i", i=4),
+        )
+        quantise(zn_codes, zn_sc, zn_tail_woven, head, V, head)
+
+        res_head = keep.tile([P, N // P, head], F32, name="res_head", align_bytes=64)
+        res_tail = keep.tile([P, N // P, CHUNK], F32, name="res_tail", align_bytes=64)
+        out_v = out.rearrange("(b p) v -> p b v", p=P)
+        for c in range(CHUNKS):
+            product(1, zn_codes, zn_sc, c)
+            for b in range(N // P):
+                res = res_head[:, b, c * CHUNK : (c + 1) * CHUNK] if c < CHUNKS - 1 else res_tail[:, b, :]
+                nc.scalar.activation(out=res, in_=accs[(b, c)][:, :CHUNK], func=TANH)
+            if c == CHUNKS - 2:
+                nc.sync.dma_start(out=out_v[:, :, :head], in_=res_head[:])
+        nc.sync.dma_start(out=out_v[:, :, head:], in_=res_tail[:])

@@ -14,6 +14,8 @@ U8 = mybir.dt.uint8
 FP8X4 = mybir.dt.float8_e4m3fn_x4
 FP4X4 = mybir.dt.float4_e2m1fn_x4
 MAX = mybir.AluOpType.max
+ADD = mybir.AluOpType.add
+SUB = mybir.AluOpType.subtract
 RELU = mybir.ActivationFunctionType.Relu
 TANH = mybir.ActivationFunctionType.Tanh
 
@@ -82,14 +84,14 @@ def tile_picked_zsgn_max_p_kernel(
             nc.scalar.copy(
                 out=dst[:, u * P // 2 : (u + 1) * P // 2], in_=w1_raw[u][:].rearrange("p j (m t) -> p m j t", t=PACK)
             )
-        w1_codes = keep.tile([P, H], U32, name="w1_codes", tag="late_a", align_bytes=64)
+        w1_codes = keep.tile([P, H], U32, name="w1_codes", align_bytes=64)
         w1_sc = keep.tile([P, H], U8, name="w1_sc", align_bytes=64)
         nc.vector.quantize_mx(
             out=w1_codes[:].bitcast(FP8X4), scales=w1_sc[:], in_=w1_bf[:].rearrange("p t m j -> p (t m j)")
         )
 
         x_codes = keep.tile([P, S], U32, name="x_codes", align_bytes=64)
-        first_pieces = [(0, 512), (512, 768), (768, 1024)]
+        first_pieces = [(0, 256), (256, 512), (512, 768), (768, 1024)]
         for a, b in first_pieces:
             nc.vector.tensor_copy(
                 x_codes[:, a:b], x_word_table[:].bitcast(U32).indirect(offs_sb[:, a // 16 : b // 16])
@@ -144,7 +146,7 @@ def tile_picked_zsgn_max_p_kernel(
             w_codes = w2_codes if which == 0 else w3_codes
             for b in range(N // P):
                 if which == 0:
-                    accs[(b, c)] = psum.tile([P, BANK], F32, name="out%d_%d" % (b, c), tag="bank%d" % ((1 + 2 * c + b) % 8))
+                    accs[(b, c)] = psum.tile([P, BANK], F32, name="out%d_%d" % (b, c), tag="bank%d" % ((2 + 2 * c + b) % 8))
                 nc.tensor.matmul_mx(
                     out=accs[(b, c)][:, :CHUNK],
                     lhsT=w_codes[:, 2 * P * b : 2 * P * (b + 1)].bitcast(FP4X4),
@@ -156,23 +158,27 @@ def tile_picked_zsgn_max_p_kernel(
                 )
 
         head = V - CHUNK
-        friend1 = keep.tile([P, CHUNKS, PACK, CHUNK], BF16, name="friend1", align_bytes=64)
-        friend2 = keep.tile([P, CHUNKS, PACK, CHUNK], BF16, name="friend2", tag="late_b", align_bytes=64)
+        half = V // 2
+        friend2 = keep.tile([P, 2, PACK, half], BF16, name="friend2", align_bytes=64)
+        zp = keep.tile([P, 2, PACK, half], BF16, name="zp", align_bytes=64)
         for t in range(PACK):
-            fetch(friend1, t, pos1_sb, 0, V)
+            friend1 = keep.tile([P, 2, half + 32], BF16, name="friend1_%d" % t, tag="late_%d" % t, align_bytes=64)
+            nc.vector.tensor_copy(friend1[:, :, :half], h[t][:].indirect(pos1_sb[:]))
             fetch(friend2, t, pos2_sb, 0, V)
-        foe1_head = keep.tile([P, CHUNKS - 1, PACK, CHUNK], BF16, name="foe1_head", tag="late_a", align_bytes=64)
-        fetch(foe1_head, 0, foe1_sb, 0, head)
-        zp = larger("zp", friend1, friend2, CHUNKS, CHUNK)
-        fetch(foe1_head, 1, foe1_sb, 0, head)
+            diff = keep.tile([P, 2, half], F32, name="diff%d" % t, align_bytes=64)
+            excess = keep.tile([P, 2, half], F32, name="excess%d" % t, align_bytes=64)
+            nc.gpsimd.tensor_tensor(diff[:], friend1[:, :, :half], friend2[:, :, t, :], SUB)
+            nc.scalar.activation(out=excess[:], in_=diff[:], func=RELU)
+            nc.gpsimd.tensor_tensor(zp[:, :, t, :], excess[:], friend2[:, :, t, :], ADD)
+        foe1_head = keep.tile([P, CHUNKS - 1, PACK, CHUNK], BF16, name="foe1_head", tag="late_2", align_bytes=64)
+        for t in range(PACK):
+            fetch(foe1_head, t, foe1_sb, 0, head)
         zp_woven = keep.tile([P, V, PACK], BF16, name="zp_woven", tag="late_c", align_bytes=64)
-        for c in range(CHUNKS):
-            weave(nc.scalar.copy, zp_woven, zp, c, CHUNK)
-        foe2_head = keep.tile([P, CHUNKS - 1, PACK, CHUNK], BF16, name="foe2_head", tag="late_b", align_bytes=64)
+        for r in range(2):
+            weave(nc.scalar.copy, zp_woven, zp, r, half)
+        foe2_head = keep.tile([P, CHUNKS - 1, PACK, CHUNK], BF16, name="foe2_head", tag="late_3", align_bytes=64)
         for t in range(PACK):
             fetch(foe2_head, t, foe2_sb, 0, head)
-            if t >= 2:
-                fetch(foe1_head, t, foe1_sb, 0, head)
         zn_head = larger("zn_head", foe1_head, foe2_head, CHUNKS - 1, CHUNK)
         zp_codes = keep.tile([P, V], U32, name="zp_codes", align_bytes=64)
         zp_sc = keep.tile([P, V], U8, name="zp_sc", align_bytes=64)

@@ -46,7 +46,7 @@ def tile_picked_zsgn_max_p_kernel(
         foe1_sb = lists.tile([P, V // 16], U16, name="foe1_sb")
         foe2_sb = lists.tile([P, V // 16], U16, name="foe2_sb")
 
-        x_scale_table = keep.tile([P, T], U8, name="x_scale_table", align_bytes=64)
+        x_scale_table = keep.tile([P, T], U8, name="x_scale_table", tag="x_first", align_bytes=64)
         nc.vector.memset(x_scale_table[:].bitcast(I32), 0)
         zero = keep.tile([P, 1], F32, name="zero")
         nc.vector.memset(zero[:], 0.0)
@@ -55,13 +55,18 @@ def tile_picked_zsgn_max_p_kernel(
 
         nc.sync.dma_start(offs_sb[:], offs)
         w1_rows = w1.rearrange("(p j) c -> p j c", j=PACK)
-        w1_raw = [keep.tile([P, PACK, H // 2], F32, name="w1_raw%d" % u, align_bytes=64) for u in range(2)]
-        nc.sync.dma_start(out=w1_raw[0][:], in_=w1_rows[:, :, : H // 2])
+        w1_parts = [(0, 256), (256, 384), (384, 512)]
+        w1_raw = [
+            keep.tile([P, PACK, b - a], F32, name="w1_raw%d" % u, tag="w1_raw%d" % u, align_bytes=64)
+            for u, (a, b) in enumerate(w1_parts)
+        ]
+        nc.sync.dma_start(out=w1_raw[0][:], in_=w1_rows[:, :, 0:256])
         nc.sync.dma_start(pos1_sb[:], pos1)
         load_scale_rows(nc.sync, x_scale_table, x_scales[0])
-        nc.sync.dma_start(out=w1_raw[1][:], in_=w1_rows[:, :, H // 2 :])
         x_word_table = keep.tile([P, T], I32, name="x_word_table", align_bytes=64)
         nc.sync.dma_start(out=x_word_table[:], in_=x_words[0].rearrange("p n t -> p (n t)").bitcast(I32))
+        nc.sync.dma_start(out=w1_raw[1][:], in_=w1_rows[:, :, 256:384])
+        nc.sync.dma_start(out=w1_raw[2][:], in_=w1_rows[:, :, 384:512])
         nc.sync.dma_start(pos2_sb[:], pos2)
         nc.sync.dma_start(foe1_sb[:], foe1)
         nc.sync.dma_start(foe2_sb[:], foe2)
@@ -80,52 +85,57 @@ def tile_picked_zsgn_max_p_kernel(
 
         w1_bf = keep.tile([P, PACK, P, PACK], BF16, name="w1_bf", align_bytes=64)
         dst = w1_bf[:].rearrange("p t m j -> p m j t")
-        for u in range(2):
+        for u, (a, b) in enumerate(w1_parts):
             nc.scalar.copy(
-                out=dst[:, u * P // 2 : (u + 1) * P // 2], in_=w1_raw[u][:].rearrange("p j (m t) -> p m j t", t=PACK)
+                out=dst[:, a // PACK : b // PACK], in_=w1_raw[u][:].rearrange("p j (m t) -> p m j t", t=PACK)
             )
-        w1_codes = keep.tile([P, H], U32, name="w1_codes", align_bytes=64)
-        w1_sc = keep.tile([P, H], U8, name="w1_sc", align_bytes=64)
-        nc.vector.quantize_mx(
-            out=w1_codes[:].bitcast(FP8X4), scales=w1_sc[:], in_=w1_bf[:].rearrange("p t m j -> p (t m j)")
-        )
+        w1_codes = keep.tile([P, PACK, P], U32, name="w1_codes", align_bytes=64)
+        w1_sc = keep.tile([P, PACK, P], U8, name="w1_sc", align_bytes=64)
 
-        x_codes = keep.tile([P, S], U32, name="x_codes", align_bytes=64)
-        first_pieces = [(0, 256), (256, 512), (512, 768), (768, 1024)]
-        for a, b in first_pieces:
-            nc.vector.tensor_copy(
-                x_codes[:, a:b], x_word_table[:].bitcast(U32).indirect(offs_sb[:, a // 16 : b // 16])
+        def quantise_w1(t0, t1):
+            nc.vector.quantize_mx(
+                out=w1_codes[:, t0:t1, :].rearrange("p t m -> p (t m)").bitcast(FP8X4),
+                scales=w1_sc[:, t0:t1, :].rearrange("p t m -> p (t m)"),
+                in_=w1_bf[:, t0:t1].rearrange("p t m j -> p (t m j)"),
             )
+
+        x_window = x_word_table[:].bitcast(U32)
+        x_codes = keep.tile([P, 768], U32, name="x_codes", tag="x_first", align_bytes=64)
+        nc.vector.tensor_copy(x_codes[:, 0:512], x_window.indirect(offs_sb[:, 0:32]))
+        nc.vector.tensor_copy(x_codes[:, 512:768], x_window.indirect(offs_sb[:, 32:48]))
+        quantise_w1(0, 1)
+        x_codes_last = keep.tile([P, 256], U32, name="x_codes_last", tag="w1_raw2", align_bytes=64)
+        nc.vector.tensor_copy(x_codes_last[:], x_window.indirect(offs_sb[:, 48:64]))
+        quantise_w1(1, 2)
+        quantise_w1(2, 4)
+        pieces = [(0, 512, x_codes[:, 0:512]), (512, 768, x_codes[:, 512:768]), (768, 1024, x_codes_last[:])]
+        quarters = [(0, 256, x_codes[:, 0:256]), (256, 512, x_codes[:, 256:512])] + pieces[1:]
 
         h = [keep.tile([P, S], F32, name="h%d" % t, align_bytes=64) for t in range(PACK)]
         bank = 0
         for t in range(PACK):
-            pieces = first_pieces if t == 0 else [(0, 512), (512, 1024)]
-            for a, b in pieces:
-                acc = psum.tile([P, BANK], F32, name="acc%d" % bank, tag="bank%d" % (bank % 8))
+            groups = [[q] for q in quarters] if t == 0 else [pieces[0:1], pieces[1:3]]
+            for group in groups:
+                acc = psum.tile([P, BANK], F32, name="acc%d" % bank, tag="bank%d" % (bank if bank < 4 else (bank - 3) % 4))
                 bank += 1
-                nc.tensor.matmul_mx(
-                    out=acc[:, : b - a],
-                    lhsT=w1_codes[:, t * P : (t + 1) * P].bitcast(FP8X4),
-                    lhsT_scale=w1_sc[:, t * P : (t + 1) * P],
-                    rhs=x_codes[:, a:b].bitcast(FP8X4),
-                    rhs_scale=x_sc[:, a:b],
-                    start=True,
-                    stop=True,
-                )
-                if t == 0 and a == 0:
-                    nc.scalar.activation(out=h[t][:, a:b], in_=acc[:, : b - a], func=RELU, bias=relu_bias[:])
+                g0, g1 = group[0][0], group[-1][1]
+                for a, b, codes in group:
+                    nc.tensor.matmul_mx(
+                        out=acc[:, a - g0 : b - g0],
+                        lhsT=w1_codes[:, t, :].bitcast(FP8X4),
+                        lhsT_scale=w1_sc[:, t, :],
+                        rhs=codes.bitcast(FP8X4),
+                        rhs_scale=x_sc[:, a:b],
+                        start=True,
+                        stop=True,
+                    )
+                if t == 0 and g0 == 0:
+                    nc.scalar.activation(out=h[t][:, g0:g1], in_=acc[:, : g1 - g0], func=RELU, bias=relu_bias[:])
                 else:
-                    nc.scalar.activation(out=h[t][:, a:b], in_=acc[:, : b - a], func=RELU)
+                    nc.scalar.activation(out=h[t][:, g0:g1], in_=acc[:, : g1 - g0], func=RELU)
 
         def fetch(dst_tile, t, list_sb, v0, v1):
             nc.vector.tensor_copy(dst_tile[:, :, t, :], h[t][:].indirect(list_sb[:, v0 // 16 : v1 // 16]))
-
-        def larger(name, a, b, runs, run):
-            z = keep.tile([P, runs, PACK, run], BF16, name=name, align_bytes=64)
-            flat = "p r t v -> p (r t v)"
-            nc.vector.tensor_tensor(z[:].rearrange(flat), a[:].rearrange(flat), b[:].rearrange(flat), MAX)
-            return z
 
         def weave(copy, woven, z, r, run):
             copy(
@@ -133,11 +143,11 @@ def tile_picked_zsgn_max_p_kernel(
                 in_=z[:, r].rearrange("p t (c i) -> p c t i", i=4),
             )
 
-        def quantise(codes, scales, woven, v0, v1, w0):
+        def quantise(codes, scales, woven, v0, v1):
             nc.vector.quantize_mx(
                 out=codes[:, v0:v1].bitcast(FP8X4),
                 scales=scales[:, v0:v1],
-                in_=woven[:, v0 - w0 : v1 - w0, :].rearrange("p v t -> p (v t)"),
+                in_=woven[:, v0:v1, :].rearrange("p v t -> p (v t)"),
             )
 
         accs = {}
@@ -146,7 +156,7 @@ def tile_picked_zsgn_max_p_kernel(
             w_codes = w2_codes if which == 0 else w3_codes
             for b in range(N // P):
                 if which == 0:
-                    accs[(b, c)] = psum.tile([P, BANK], F32, name="out%d_%d" % (b, c), tag="bank%d" % ((2 + 2 * c + b) % 8))
+                    accs[(b, c)] = psum.tile([P, BANK], F32, name="out%d_%d" % (b, c), tag="bank%d" % (2 * c + b))
                 nc.tensor.matmul_mx(
                     out=accs[(b, c)][:, :CHUNK],
                     lhsT=w_codes[:, 2 * P * b : 2 * P * (b + 1)].bitcast(FP4X4),
@@ -160,7 +170,7 @@ def tile_picked_zsgn_max_p_kernel(
         head = V - CHUNK
         half = V // 2
         friend2 = keep.tile([P, 2, PACK, half], BF16, name="friend2", align_bytes=64)
-        zp = keep.tile([P, 2, PACK, half], BF16, name="zp", align_bytes=64)
+        zp = keep.tile([P, 2, PACK, half], BF16, name="zp", tag="late_d", align_bytes=64)
         for t in range(PACK):
             friend1 = keep.tile([P, 2, half + 32], BF16, name="friend1_%d" % t, tag="late_%d" % t, align_bytes=64)
             nc.vector.tensor_copy(friend1[:, :, :half], h[t][:].indirect(pos1_sb[:]))
@@ -170,49 +180,57 @@ def tile_picked_zsgn_max_p_kernel(
             nc.gpsimd.tensor_tensor(diff[:], friend1[:, :, :half], friend2[:, :, t, :], SUB)
             nc.scalar.activation(out=excess[:], in_=diff[:], func=RELU)
             nc.gpsimd.tensor_tensor(zp[:, :, t, :], excess[:], friend2[:, :, t, :], ADD)
-        foe1_head = keep.tile([P, CHUNKS - 1, PACK, CHUNK], BF16, name="foe1_head", tag="late_2", align_bytes=64)
-        for t in range(PACK):
-            fetch(foe1_head, t, foe1_sb, 0, head)
         zp_woven = keep.tile([P, V, PACK], BF16, name="zp_woven", tag="late_c", align_bytes=64)
         for r in range(2):
             weave(nc.scalar.copy, zp_woven, zp, r, half)
-        foe2_head = keep.tile([P, CHUNKS - 1, PACK, CHUNK], BF16, name="foe2_head", tag="late_3", align_bytes=64)
+
+        last = PACK - 1
+        tail = CHUNKS - 1
+        foes1 = keep.tile([P, CHUNKS, PACK, CHUNK], BF16, name="foes1", tag="late_2", align_bytes=64)
+        foes2 = keep.tile([P, CHUNKS, PACK, CHUNK], BF16, name="foes2", tag="late_3", align_bytes=64)
         for t in range(PACK):
-            fetch(foe2_head, t, foe2_sb, 0, head)
-        zn_head = larger("zn_head", foe1_head, foe2_head, CHUNKS - 1, CHUNK)
+            fetch(foes1, t, foe1_sb, 0, V)
+        for t in range(last):
+            fetch(foes2, t, foe2_sb, 0, V)
+        fetch(foes2[:, :tail], last, foe2_sb, 0, head)
         zp_codes = keep.tile([P, V], U32, name="zp_codes", align_bytes=64)
         zp_sc = keep.tile([P, V], U8, name="zp_sc", align_bytes=64)
-        quantise(zp_codes, zp_sc, zp_woven, 0, V, 0)
+        quantise(zp_codes, zp_sc, zp_woven, 0, V)
         for c in range(CHUNKS):
             product(0, zp_codes, zp_sc, c)
-        zn_head_woven = keep.tile([P, head, PACK], BF16, name="zn_head_woven", align_bytes=64)
-        for c in range(CHUNKS - 1):
-            weave(nc.scalar.copy, zn_head_woven, zn_head, c, CHUNK)
+        zn = keep.tile([P, CHUNKS, PACK, CHUNK], BF16, name="zn", tag="late_d", align_bytes=64)
+        zn_woven = keep.tile([P, V, PACK], BF16, name="zn_woven", align_bytes=64)
+        for c in range(tail):
+            nc.vector.tensor_tensor(zn[:, c], foes1[:, c], foes2[:, c], MAX)
+            weave(nc.scalar.copy, zn_woven, zn, c, CHUNK)
+        nc.vector.tensor_tensor(zn[:, tail, :last, :], foes1[:, tail, :last, :], foes2[:, tail, :last, :], MAX)
 
-        foes_tail = keep.tile([P, 2, 2, PACK, CHUNK // 2], BF16, name="foes_tail", tag="late_c", align_bytes=64)
-        for t in range(PACK):
-            fetch(foes_tail[:, 0], t, foe1_sb, head, V)
-            fetch(foes_tail[:, 1], t, foe2_sb, head, V)
+        foes2_tail = keep.tile([P, 2, CHUNK], BF16, name="foes2_tail", tag="late_c", align_bytes=64)
+        nc.vector.tensor_copy(foes2_tail[:, :, : CHUNK // 2], h[last][:].indirect(foe2_sb[:, head // 16 :]))
         zn_codes = keep.tile([P, V], U32, name="zn_codes", align_bytes=64)
         zn_sc = keep.tile([P, V], U8, name="zn_sc", align_bytes=64)
-        quantise(zn_codes, zn_sc, zn_head_woven, 0, 256, 0)
-        zn_tail = larger("zn_tail", foes_tail[:, 0], foes_tail[:, 1], 2, CHUNK // 2)
-        quantise(zn_codes, zn_sc, zn_head_woven, 256, head, 0)
-        zn_tail_woven = keep.tile([P, CHUNK, PACK], BF16, name="zn_tail_woven", align_bytes=64)
-        nc.vector.tensor_copy(
-            out=zn_tail_woven[:].rearrange("p (r c i) t -> p r c t i", r=2, i=4),
-            in_=zn_tail[:].rearrange("p r t (c i) -> p r c t i", i=4),
+        quantise(zn_codes, zn_sc, zn_woven, 0, CHUNK)
+        nc.vector.tensor_tensor(
+            zn[:, tail, last, :].rearrange("p (r v) -> p r v", r=2),
+            foes1[:, tail, last, :].rearrange("p (r v) -> p r v", r=2),
+            foes2_tail[:, :, : CHUNK // 2],
+            MAX,
         )
-        quantise(zn_codes, zn_sc, zn_tail_woven, head, V, head)
+        quantise(zn_codes, zn_sc, zn_woven, CHUNK, 2 * CHUNK)
+        weave(nc.vector.tensor_copy, zn_woven, zn, tail, CHUNK)
+        quantise(zn_codes, zn_sc, zn_woven, 2 * CHUNK, head)
+        quantise(zn_codes, zn_sc, zn_woven, head, V)
 
-        res_head = keep.tile([P, N // P, head], F32, name="res_head", align_bytes=64)
-        res_tail = keep.tile([P, N // P, CHUNK], F32, name="res_tail", align_bytes=64)
+        res = keep.tile([P, N // P, V], F32, name="res", align_bytes=64)
         out_v = out.rearrange("(b p) v -> p b v", p=P)
+        stored = 0
         for c in range(CHUNKS):
             product(1, zn_codes, zn_sc, c)
             for b in range(N // P):
-                res = res_head[:, b, c * CHUNK : (c + 1) * CHUNK] if c < CHUNKS - 1 else res_tail[:, b, :]
-                nc.scalar.activation(out=res, in_=accs[(b, c)][:, :CHUNK], func=TANH)
-            if c == CHUNKS - 2:
-                nc.sync.dma_start(out=out_v[:, :, :head], in_=res_head[:])
-        nc.sync.dma_start(out=out_v[:, :, head:], in_=res_tail[:])
+                nc.scalar.activation(
+                    out=res[:, b, c * CHUNK : (c + 1) * CHUNK], in_=accs[(b, c)][:, :CHUNK], func=TANH
+                )
+            if c >= 1:
+                done = (c + 1) * CHUNK
+                nc.sync.dma_start(out=out_v[:, :, stored:done], in_=res[:, :, stored:done])
+                stored = done

@@ -137,10 +137,10 @@ def tile_picked_zsgn_max_p_kernel(
         def fetch(dst_tile, t, list_sb, v0, v1):
             nc.vector.tensor_copy(dst_tile[:, :, t, :], h[t][:].indirect(list_sb[:, v0 // 16 : v1 // 16]))
 
-        def weave(copy, woven, z, r, run):
+        def weave(copy, woven, planes):
             copy(
-                out=woven[:, r * run : (r + 1) * run, :].rearrange("p (c i) t -> p c t i", i=4),
-                in_=z[:, r].rearrange("p t (c i) -> p c t i", i=4),
+                out=woven.rearrange("p (c i) t -> p c t i", i=4),
+                in_=planes.rearrange("p t (c i) -> p c t i", i=4),
             )
 
         def quantise(codes, scales, woven, v0, v1):
@@ -169,20 +169,20 @@ def tile_picked_zsgn_max_p_kernel(
 
         head = V - CHUNK
         half = V // 2
-        friend2 = keep.tile([P, 2, PACK, half], BF16, name="friend2", align_bytes=64)
-        zp = keep.tile([P, 2, PACK, half], BF16, name="zp", tag="late_d", align_bytes=64)
+        zp = keep.tile([P, PACK, V], BF16, name="zp", tag="late_d", align_bytes=64)
         for t in range(PACK):
-            friend1 = keep.tile([P, 2, half + 32], BF16, name="friend1_%d" % t, tag="late_%d" % t, align_bytes=64)
-            nc.vector.tensor_copy(friend1[:, :, :half], h[t][:].indirect(pos1_sb[:]))
-            fetch(friend2, t, pos2_sb, 0, V)
-            diff = keep.tile([P, 2, half], F32, name="diff%d" % t, align_bytes=64)
-            excess = keep.tile([P, 2, half], F32, name="excess%d" % t, align_bytes=64)
-            nc.gpsimd.tensor_tensor(diff[:], friend1[:, :, :half], friend2[:, :, t, :], SUB)
+            friend1 = keep.tile([P, V], F32, name="friend1_%d" % t, tag="late_%d" % t, align_bytes=64)
+            friend2 = keep.tile([P, V], F32, name="friend2_%d" % t, align_bytes=64)
+            nc.vector.tensor_copy(friend1[:], h[t][:].indirect(pos1_sb[:]))
+            nc.vector.tensor_copy(friend2[:], h[t][:].indirect(pos2_sb[:]))
+            diff = keep.tile([P, V], F32, name="diff%d" % t, align_bytes=64)
+            excess = keep.tile([P, V], F32, name="excess%d" % t, align_bytes=64)
+            nc.gpsimd.tensor_tensor(diff[:], friend1[:], friend2[:], SUB)
             nc.scalar.activation(out=excess[:], in_=diff[:], func=RELU)
-            nc.gpsimd.tensor_tensor(zp[:, :, t, :], excess[:], friend2[:, :, t, :], ADD)
+            nc.gpsimd.tensor_tensor(zp[:, t, :], excess[:], friend2[:], ADD)
         zp_woven = keep.tile([P, V, PACK], BF16, name="zp_woven", tag="late_c", align_bytes=64)
-        for r in range(2):
-            weave(nc.scalar.copy, zp_woven, zp, r, half)
+        for v0 in (0, half):
+            weave(nc.scalar.copy, zp_woven[:, v0 : v0 + half, :], zp[:, :, v0 : v0 + half])
 
         last = PACK - 1
         tail = CHUNKS - 1
@@ -202,7 +202,7 @@ def tile_picked_zsgn_max_p_kernel(
         zn_woven = keep.tile([P, V, PACK], BF16, name="zn_woven", align_bytes=64)
         for c in range(tail):
             nc.vector.tensor_tensor(zn[:, c], foes1[:, c], foes2[:, c], MAX)
-            weave(nc.scalar.copy, zn_woven, zn, c, CHUNK)
+            weave(nc.scalar.copy, zn_woven[:, c * CHUNK : (c + 1) * CHUNK, :], zn[:, c])
         nc.vector.tensor_tensor(zn[:, tail, :last, :], foes1[:, tail, :last, :], foes2[:, tail, :last, :], MAX)
 
         foes2_tail = keep.tile([P, 2, CHUNK], BF16, name="foes2_tail", tag="late_c", align_bytes=64)
@@ -217,7 +217,7 @@ def tile_picked_zsgn_max_p_kernel(
             MAX,
         )
         quantise(zn_codes, zn_sc, zn_woven, CHUNK, 2 * CHUNK)
-        weave(nc.vector.tensor_copy, zn_woven, zn, tail, CHUNK)
+        weave(nc.vector.tensor_copy, zn_woven[:, head:, :], zn[:, tail])
         quantise(zn_codes, zn_sc, zn_woven, 2 * CHUNK, head)
         quantise(zn_codes, zn_sc, zn_woven, head, V)
 
@@ -230,7 +230,9 @@ def tile_picked_zsgn_max_p_kernel(
                 nc.scalar.activation(
                     out=res[:, b, c * CHUNK : (c + 1) * CHUNK], in_=accs[(b, c)][:, :CHUNK], func=TANH
                 )
-            if c >= 1:
+                if c == tail:
+                    nc.sync.dma_start(out=out_v[:, b, head:], in_=res[:, b, head:])
+            if 1 <= c < tail:
                 done = (c + 1) * CHUNK
                 nc.sync.dma_start(out=out_v[:, :, stored:done], in_=res[:, :, stored:done])
                 stored = done

@@ -46,7 +46,7 @@ def tile_picked_zsgn_max_p_kernel(
         foe1_sb = lists.tile([P, V // 16], U16, name="foe1_sb")
         foe2_sb = lists.tile([P, V // 16], U16, name="foe2_sb")
 
-        x_scale_table = keep.tile([P, T], U8, name="x_scale_table", tag="x_first", align_bytes=64)
+        x_scale_table = keep.tile([P, T], U8, name="x_scale_table", align_bytes=64)
         nc.vector.memset(x_scale_table[:].bitcast(I32), 0)
         zero = keep.tile([P, 1], F32, name="zero")
         nc.vector.memset(zero[:], 0.0)
@@ -55,18 +55,18 @@ def tile_picked_zsgn_max_p_kernel(
 
         nc.sync.dma_start(offs_sb[:], offs)
         w1_rows = w1.rearrange("(p j) c -> p j c", j=PACK)
-        w1_parts = [(0, 256), (256, 384), (384, 512)]
+        w1_parts = [(0, 128), (128, 256), (256, 384), (384, 512)]
         w1_raw = [
             keep.tile([P, PACK, b - a], F32, name="w1_raw%d" % u, tag="w1_raw%d" % u, align_bytes=64)
             for u, (a, b) in enumerate(w1_parts)
         ]
-        nc.sync.dma_start(out=w1_raw[0][:], in_=w1_rows[:, :, 0:256])
+        nc.sync.dma_start(out=w1_raw[0][:], in_=w1_rows[:, :, 0:128])
         nc.sync.dma_start(pos1_sb[:], pos1)
         load_scale_rows(nc.sync, x_scale_table, x_scales[0])
         x_word_table = keep.tile([P, T], I32, name="x_word_table", align_bytes=64)
         nc.sync.dma_start(out=x_word_table[:], in_=x_words[0].rearrange("p n t -> p (n t)").bitcast(I32))
-        nc.sync.dma_start(out=w1_raw[1][:], in_=w1_rows[:, :, 256:384])
-        nc.sync.dma_start(out=w1_raw[2][:], in_=w1_rows[:, :, 384:512])
+        for u in range(1, 4):
+            nc.sync.dma_start(out=w1_raw[u][:], in_=w1_rows[:, :, w1_parts[u][0] : w1_parts[u][1]])
         nc.sync.dma_start(pos2_sb[:], pos2)
         nc.sync.dma_start(foe1_sb[:], foe1)
         nc.sync.dma_start(foe2_sb[:], foe2)
@@ -85,10 +85,10 @@ def tile_picked_zsgn_max_p_kernel(
 
         w1_bf = keep.tile([P, PACK, P, PACK], BF16, name="w1_bf", align_bytes=64)
         dst = w1_bf[:].rearrange("p t m j -> p m j t")
-        for u, (a, b) in enumerate(w1_parts):
-            nc.scalar.copy(
-                out=dst[:, a // PACK : b // PACK], in_=w1_raw[u][:].rearrange("p j (m t) -> p m j t", t=PACK)
-            )
+        srcs = [w1_raw[u][:].rearrange("p j (m t) -> p m j t", t=PACK) for u in range(4)]
+        for u in range(3):
+            nc.scalar.copy(out=dst[:, 32 * u : 32 * (u + 1)], in_=srcs[u])
+        nc.scalar.copy(out=dst[:, 96:112], in_=srcs[3][:, :16])
         w1_codes = keep.tile([P, PACK, P], U32, name="w1_codes", align_bytes=64)
         w1_sc = keep.tile([P, PACK, P], U8, name="w1_sc", align_bytes=64)
 
@@ -100,11 +100,12 @@ def tile_picked_zsgn_max_p_kernel(
             )
 
         x_window = x_word_table[:].bitcast(U32)
-        x_codes = keep.tile([P, 768], U32, name="x_codes", tag="x_first", align_bytes=64)
+        x_codes = keep.tile([P, 768], U32, name="x_codes", align_bytes=64)
         nc.vector.tensor_copy(x_codes[:, 0:512], x_window.indirect(offs_sb[:, 0:32]))
         nc.vector.tensor_copy(x_codes[:, 512:768], x_window.indirect(offs_sb[:, 32:48]))
+        nc.vector.tensor_copy(out=dst[:, 112:128], in_=srcs[3][:, 16:])
         quantise_w1(0, 1)
-        x_codes_last = keep.tile([P, 256], U32, name="x_codes_last", tag="w1_raw2", align_bytes=64)
+        x_codes_last = keep.tile([P, 256], U32, name="x_codes_last", tag="w1_raw3", align_bytes=64)
         nc.vector.tensor_copy(x_codes_last[:], x_window.indirect(offs_sb[:, 48:64]))
         quantise_w1(1, 2)
         quantise_w1(2, 4)

@@ -171,16 +171,31 @@ def tile_picked_zsgn_max_p_kernel(
         head = V - CHUNK
         half = V // 2
         zp = keep.tile([P, PACK, V], BF16, name="zp", tag="late_d", align_bytes=64)
+        def larger_begin(name, first, second, tag):
+            diff = keep.tile([P, V], F32, name="diff" + name, tag=tag, align_bytes=64)
+            nc.gpsimd.tensor_tensor(diff[:], first, second, SUB)
+            return diff
+
+        def larger_end(name, diff, second, dst_plane):
+            excess = keep.tile([P, V], F32, name="excess" + name, tag="excess" + name, align_bytes=64)
+            nc.scalar.activation(out=excess[:], in_=diff[:], func=RELU)
+            nc.gpsimd.tensor_tensor(dst_plane, excess[:], second, ADD)
+
+        diff_slots = ["diff0", "excess0", "late_1", "excess1"]
+        pending = None
         for t in range(PACK):
             friend1 = keep.tile([P, V], F32, name="friend1_%d" % t, tag="late_%d" % t, align_bytes=64)
             friend2 = keep.tile([P, V], F32, name="friend2_%d" % t, align_bytes=64)
             nc.vector.tensor_copy(friend1[:], h[t][:].indirect(pos1_sb[:]))
             nc.vector.tensor_copy(friend2[:], h[t][:].indirect(pos2_sb[:]))
-            diff = keep.tile([P, V], F32, name="diff%d" % t, align_bytes=64)
-            excess = keep.tile([P, V], F32, name="excess%d" % t, align_bytes=64)
-            nc.gpsimd.tensor_tensor(diff[:], friend1[:], friend2[:], SUB)
-            nc.scalar.activation(out=excess[:], in_=diff[:], func=RELU)
-            nc.gpsimd.tensor_tensor(zp[:, t, :], excess[:], friend2[:], ADD)
+            diff = larger_begin("%d" % t, friend1[:], friend2[:], diff_slots[t])
+            if pending is not None:
+                larger_end(*pending)
+            pending = ("%d" % t, diff, friend2[:], zp[:, t, :])
+            if t == 0:
+                larger_end(*pending)
+                pending = None
+        larger_end(*pending)
         zp_woven = keep.tile([P, V, PACK], BF16, name="zp_woven", tag="late_c", align_bytes=64)
         for v0 in (0, half):
             weave(nc.scalar.copy, zp_woven[:, v0 : v0 + half, :], zp[:, :, v0 : v0 + half])
@@ -191,49 +206,51 @@ def tile_picked_zsgn_max_p_kernel(
         foes2 = keep.tile([P, CHUNKS, PACK, CHUNK], BF16, name="foes2", tag="late_3", align_bytes=64)
         for t in range(PACK):
             fetch(foes1, t, foe1_sb, 0, V)
-        for t in range(last):
+        for t in range(2):
             fetch(foes2, t, foe2_sb, 0, V)
-        fetch(foes2[:, :tail], last, foe2_sb, 0, head)
+        for t in range(2, PACK):
+            fetch(foes2[:, :tail], t, foe2_sb, 0, head)
+        tail1 = keep.tile([P, CHUNK, PACK], BF16, name="tail1", tag="excess1", align_bytes=64)
+        weave(nc.scalar.copy, tail1[:], foes1[:, tail])
         zp_codes = keep.tile([P, V], U32, name="zp_codes", align_bytes=64)
         zp_sc = keep.tile([P, V], U8, name="zp_sc", align_bytes=64)
-        quantise(zp_codes, zp_sc, zp_woven, 0, V)
-        for c in range(CHUNKS):
+        quantise(zp_codes, zp_sc, zp_woven, 0, half)
+        for c in range(CHUNKS // 2):
             product(0, zp_codes, zp_sc, c)
-        zn = keep.tile([P, CHUNKS, PACK, CHUNK], BF16, name="zn", tag="late_d", align_bytes=64)
-        zn_woven = keep.tile([P, V, PACK], BF16, name="zn_woven", align_bytes=64)
-        for c in range(tail):
-            nc.vector.tensor_tensor(zn[:, c], foes1[:, c], foes2[:, c], MAX)
-            weave(nc.scalar.copy, zn_woven[:, c * CHUNK : (c + 1) * CHUNK, :], zn[:, c])
-        nc.vector.tensor_tensor(zn[:, tail, :last, :], foes1[:, tail, :last, :], foes2[:, tail, :last, :], MAX)
-
-        foes2_tail = keep.tile([P, 2, CHUNK], BF16, name="foes2_tail", tag="late_c", align_bytes=64)
-        nc.vector.tensor_copy(foes2_tail[:, :, : CHUNK // 2], h[last][:].indirect(foe2_sb[:, head // 16 :]))
+        zn = keep.tile([P, CHUNKS, PACK * CHUNK], BF16, name="zn", tag="late_d", align_bytes=64)
+        tail2 = zn[:, tail, :].rearrange("p (v t) -> p v t", t=PACK)
+        weave(nc.scalar.copy, tail2[:, :, :2], foes2[:, tail, :2, :])
+        zn_woven = keep.tile([P, head, PACK], BF16, name="zn_woven", align_bytes=64)
         zn_codes = keep.tile([P, V], U32, name="zn_codes", align_bytes=64)
         zn_sc = keep.tile([P, V], U8, name="zn_sc", align_bytes=64)
+
+        def larger_foes(c):
+            planes = zn[:, c, :].rearrange("p (t v) -> p t v", t=PACK)
+            nc.vector.tensor_tensor(planes, foes1[:, c], foes2[:, c], MAX)
+            weave(nc.scalar.copy, zn_woven[:, c * CHUNK : (c + 1) * CHUNK, :], planes)
+
+        larger_foes(0)
+        larger_foes(1)
+        quantise(zp_codes, zp_sc, zp_woven, half, V)
+        for c in range(CHUNKS // 2, CHUNKS):
+            product(0, zp_codes, zp_sc, c)
+        larger_foes(2)
         quantise(zn_codes, zn_sc, zn_woven, 0, CHUNK)
-        nc.vector.tensor_tensor(
-            zn[:, tail, last, :].rearrange("p (r v) -> p r v", r=2),
-            foes1[:, tail, last, :].rearrange("p (r v) -> p r v", r=2),
-            foes2_tail[:, :, : CHUNK // 2],
-            MAX,
-        )
+        nc.vector.tensor_copy(tail2[:, :, 2], h[2][:].indirect(foe2_sb[:, head // 16 :]))
+        nc.vector.tensor_copy(tail2[:, :, 3], h[3][:].indirect(foe2_sb[:, head // 16 :]))
         quantise(zn_codes, zn_sc, zn_woven, CHUNK, 2 * CHUNK)
-        weave(nc.vector.tensor_copy, zn_woven[:, head:, :], zn[:, tail])
+        nc.vector.tensor_tensor(zn[:, 1, :], tail1[:].rearrange("p v t -> p (v t)"), zn[:, tail, :], MAX)
+        nc.vector.quantize_mx(out=zn_codes[:, head:].bitcast(FP8X4), scales=zn_sc[:, head:], in_=zn[:, 1, :])
         quantise(zn_codes, zn_sc, zn_woven, 2 * CHUNK, head)
-        quantise(zn_codes, zn_sc, zn_woven, head, V)
 
         res = keep.tile([P, N // P, V], F32, name="res", align_bytes=64)
         out_v = out.rearrange("(b p) v -> p b v", p=P)
-        stored = 0
-        for c in range(CHUNKS):
+        for c in (0, 1, 3, 2):
+            cols = slice(c * CHUNK, (c + 1) * CHUNK)
             product(1, zn_codes, zn_sc, c)
             for b in range(N // P):
-                nc.scalar.activation(
-                    out=res[:, b, c * CHUNK : (c + 1) * CHUNK], in_=accs[(b, c)][:, :CHUNK], func=TANH
-                )
-                if c == tail:
-                    nc.sync.dma_start(out=out_v[:, b, head:], in_=res[:, b, head:])
-            if 1 <= c < tail:
-                done = (c + 1) * CHUNK
-                nc.sync.dma_start(out=out_v[:, :, stored:done], in_=res[:, :, stored:done])
-                stored = done
+                nc.scalar.activation(out=res[:, b, cols], in_=accs[(b, c)][:, :CHUNK], func=TANH)
+                if c == 2:
+                    (nc.sync if b == 0 else nc.scalar).dma_start(out=out_v[:, b, cols], in_=res[:, b, cols])
+            if c != 2:
+                nc.sync.dma_start(out=out_v[:, :, cols], in_=res[:, :, cols])

@@ -101,8 +101,7 @@ def tile_picked_zsgn_max_p_kernel(
 
         x_window = x_word_table[:].bitcast(U32)
         x_codes = keep.tile([P, 768], U32, name="x_codes", align_bytes=64)
-        nc.vector.tensor_copy(x_codes[:, 0:512], x_window.indirect(offs_sb[:, 0:32]))
-        nc.vector.tensor_copy(x_codes[:, 512:768], x_window.indirect(offs_sb[:, 32:48]))
+        nc.vector.tensor_copy(x_codes[:], x_window.indirect(offs_sb[:, 0:48]))
         nc.vector.tensor_copy(out=dst[:, 112:128], in_=srcs[3][:, 16:])
         quantise_w1(0, 1)
         x_codes_last = keep.tile([P, 256], U32, name="x_codes_last", tag="w1_raw3", align_bytes=64)
@@ -206,20 +205,20 @@ def tile_picked_zsgn_max_p_kernel(
         foes2 = keep.tile([P, CHUNKS, PACK, CHUNK], BF16, name="foes2", tag="late_3", align_bytes=64)
         for t in range(PACK):
             fetch(foes1, t, foe1_sb, 0, V)
-        for t in range(2):
+        for t in range(last):
             fetch(foes2, t, foe2_sb, 0, V)
-        for t in range(2, PACK):
-            fetch(foes2[:, :tail], t, foe2_sb, 0, head)
-        tail1 = keep.tile([P, CHUNK, PACK], BF16, name="tail1", tag="excess1", align_bytes=64)
-        weave(nc.scalar.copy, tail1[:], foes1[:, tail])
+        fetch(foes2[:, :tail], last, foe2_sb, 0, head)
+        nc.scalar.copy(out=foes2[:, tail, last, :], in_=foes1[:, tail, last, :])
         zp_codes = keep.tile([P, V], U32, name="zp_codes", align_bytes=64)
         zp_sc = keep.tile([P, V], U8, name="zp_sc", align_bytes=64)
         quantise(zp_codes, zp_sc, zp_woven, 0, half)
         for c in range(CHUNKS // 2):
             product(0, zp_codes, zp_sc, c)
-        zn = keep.tile([P, CHUNKS, PACK * CHUNK], BF16, name="zn", tag="late_d", align_bytes=64)
+        zn = keep.tile([P, CHUNKS + 1, PACK * CHUNK], BF16, name="zn", tag="late_d", align_bytes=64)
         tail2 = zn[:, tail, :].rearrange("p (v t) -> p v t", t=PACK)
-        weave(nc.scalar.copy, tail2[:, :, :2], foes2[:, tail, :2, :])
+        tail1 = zn[:, tail + 1, :].rearrange("p (v t) -> p v t", t=PACK)
+        weave(nc.scalar.copy, tail1, foes1[:, tail])
+        weave(nc.scalar.copy, tail2, foes2[:, tail])
         zn_woven = keep.tile([P, head, PACK], BF16, name="zn_woven", align_bytes=64)
         zn_codes = keep.tile([P, V], U32, name="zn_codes", align_bytes=64)
         zn_sc = keep.tile([P, V], U8, name="zn_sc", align_bytes=64)
@@ -236,21 +235,20 @@ def tile_picked_zsgn_max_p_kernel(
             product(0, zp_codes, zp_sc, c)
         larger_foes(2)
         quantise(zn_codes, zn_sc, zn_woven, 0, CHUNK)
-        nc.vector.tensor_copy(tail2[:, :, 2], h[2][:].indirect(foe2_sb[:, head // 16 :]))
-        nc.vector.tensor_copy(tail2[:, :, 3], h[3][:].indirect(foe2_sb[:, head // 16 :]))
+        nc.vector.tensor_copy(tail1[:, :, 3], h[3][:].indirect(foe2_sb[:, head // 16 :]))
         quantise(zn_codes, zn_sc, zn_woven, CHUNK, 2 * CHUNK)
-        nc.vector.tensor_tensor(zn[:, 1, :], tail1[:].rearrange("p v t -> p (v t)"), zn[:, tail, :], MAX)
-        nc.vector.quantize_mx(out=zn_codes[:, head:].bitcast(FP8X4), scales=zn_sc[:, head:], in_=zn[:, 1, :])
+        nc.vector.tensor_tensor(zn[:, 1, :], zn[:, tail + 1, :], zn[:, tail, :], MAX)
         quantise(zn_codes, zn_sc, zn_woven, 2 * CHUNK, head)
+        nc.vector.quantize_mx(out=zn_codes[:, head:].bitcast(FP8X4), scales=zn_sc[:, head:], in_=zn[:, 1, :])
 
         res = keep.tile([P, N // P, V], F32, name="res", align_bytes=64)
         out_v = out.rearrange("(b p) v -> p b v", p=P)
-        for c in (0, 1, 3, 2):
+        for c in range(CHUNKS):
             cols = slice(c * CHUNK, (c + 1) * CHUNK)
             product(1, zn_codes, zn_sc, c)
             for b in range(N // P):
                 nc.scalar.activation(out=res[:, b, cols], in_=accs[(b, c)][:, :CHUNK], func=TANH)
-                if c == 2:
-                    (nc.sync if b == 0 else nc.scalar).dma_start(out=out_v[:, b, cols], in_=res[:, b, cols])
-            if c != 2:
+                if c == tail:
+                    nc.sync.dma_start(out=out_v[:, b, cols], in_=res[:, b, cols])
+            if c != tail:
                 nc.sync.dma_start(out=out_v[:, :, cols], in_=res[:, :, cols])

@@ -17,6 +17,7 @@ MAX = mybir.AluOpType.max
 ADD = mybir.AluOpType.add
 SUB = mybir.AluOpType.subtract
 RELU = mybir.ActivationFunctionType.Relu
+IDENTITY = mybir.ActivationFunctionType.Identity
 TANH = mybir.ActivationFunctionType.Tanh
 
 P = 128
@@ -77,18 +78,19 @@ def tile_picked_zsgn_max_p_kernel(
         load_scale_rows(nc.sync, w23_scales[:, 0, :], w2_scales[0])
         load_scale_rows(nc.sync, w23_scales[:, 1, :], w3_scales[0])
 
-        relu_bias = keep.tile([P, 1], F32, name="relu_bias")
+        relu_bias = keep.tile([P, 1], F32, name="relu_bias", tag="held", align_bytes=64)
         nc.scalar.activation(out=relu_bias[:], in_=zero[:], func=TANH)
 
         x_sc = keep.tile([P, S], U8, name="x_sc", align_bytes=64)
         nc.vector.tensor_copy(x_sc[:], x_scale_table[:].indirect(offs_sb[:]))
 
-        w1_bf = keep.tile([P, PACK, P, PACK], BF16, name="w1_bf", align_bytes=64)
-        dst = w1_bf[:].rearrange("p t m j -> p m j t")
+        w1_bf = keep.tile([P, PACK * P * PACK], BF16, name="w1_bf", align_bytes=64)
+        dst = w1_bf[:].rearrange("p (t m j) -> p m j t", t=PACK, j=PACK)
         srcs = [w1_raw[u][:].rearrange("p j (m t) -> p m j t", t=PACK) for u in range(4)]
         for u in range(3):
             nc.scalar.copy(out=dst[:, 32 * u : 32 * (u + 1)], in_=srcs[u])
-        nc.scalar.copy(out=dst[:, 96:112], in_=srcs[3][:, :16])
+        nc.scalar.activation(out=dst[:, 96:128, :, 0], in_=srcs[3][:, :, :, 0], func=IDENTITY, bias=relu_bias[:])
+        nc.scalar.copy(out=dst[:, 96:128, :, 1:4], in_=srcs[3][:, :, :, 1:4])
         w1_codes = keep.tile([P, PACK, P], U32, name="w1_codes", align_bytes=64)
         w1_sc = keep.tile([P, PACK, P], U8, name="w1_sc", align_bytes=64)
 
@@ -96,43 +98,47 @@ def tile_picked_zsgn_max_p_kernel(
             nc.vector.quantize_mx(
                 out=w1_codes[:, t0:t1, :].rearrange("p t m -> p (t m)").bitcast(FP8X4),
                 scales=w1_sc[:, t0:t1, :].rearrange("p t m -> p (t m)"),
-                in_=w1_bf[:, t0:t1].rearrange("p t m j -> p (t m j)"),
+                in_=w1_bf[:, t0 * P * PACK : t1 * P * PACK],
             )
 
         x_window = x_word_table[:].bitcast(U32)
-        x_codes = keep.tile([P, 768], U32, name="x_codes", align_bytes=64)
-        nc.vector.tensor_copy(x_codes[:], x_window.indirect(offs_sb[:, 0:48]))
-        nc.vector.tensor_copy(out=dst[:, 112:128], in_=srcs[3][:, 16:])
+        x_first = keep.tile([P, 768], U32, name="x_first", align_bytes=64)
+        nc.vector.tensor_copy(x_first[:], x_window.indirect(offs_sb[:, 0:48]))
         quantise_w1(0, 1)
-        x_codes_last = keep.tile([P, 256], U32, name="x_codes_last", tag="w1_raw3", align_bytes=64)
-        nc.vector.tensor_copy(x_codes_last[:], x_window.indirect(offs_sb[:, 48:64]))
+        x_rest = keep.tile([P, 256], U32, name="x_rest", tag="held", align_bytes=64)
+        nc.vector.tensor_copy(x_rest[:], x_window.indirect(offs_sb[:, 48:64]))
         quantise_w1(1, 2)
         quantise_w1(2, 4)
-        pieces = [(0, 512, x_codes[:, 0:512]), (512, 768, x_codes[:, 512:768]), (768, 1024, x_codes_last[:])]
-        quarters = [(0, 256, x_codes[:, 0:256]), (256, 512, x_codes[:, 256:512])] + pieces[1:]
+
+        def picked(a, b):
+            return x_first[:, a:b] if b <= 768 else x_rest[:, a - 768 : b - 768]
 
         h = [keep.tile([P, S], F32, name="h%d" % t, align_bytes=64) for t in range(PACK)]
         bank = 0
+        first_groups = [[(0, 256)], [(256, 512)], [(512, 768)], [(768, 896)], [(896, 1024)]]
+        later_groups = [[(0, 512)], [(512, 768), (768, 1024)]]
         for t in range(PACK):
-            groups = [[q] for q in quarters] if t == 0 else [pieces[0:1], pieces[1:3]]
-            for group in groups:
-                acc = psum.tile([P, BANK], F32, name="acc%d" % bank, tag="bank%d" % (bank if bank < 4 else (bank - 3) % 4))
+            for g, group in enumerate(first_groups if t == 0 else later_groups):
+                acc = psum.tile([P, BANK], F32, name="acc%d" % bank, tag="bank%d" % (bank % 5))
                 bank += 1
-                g0, g1 = group[0][0], group[-1][1]
-                for a, b, codes in group:
+                at = 0
+                for a, b in group:
                     nc.tensor.matmul_mx(
-                        out=acc[:, a - g0 : b - g0],
+                        out=acc[:, at : at + b - a],
                         lhsT=w1_codes[:, t, :].bitcast(FP8X4),
                         lhsT_scale=w1_sc[:, t, :],
-                        rhs=codes.bitcast(FP8X4),
+                        rhs=picked(a, b).bitcast(FP8X4),
                         rhs_scale=x_sc[:, a:b],
                         start=True,
                         stop=True,
                     )
-                if t == 0 and g0 == 0:
-                    nc.scalar.activation(out=h[t][:, g0:g1], in_=acc[:, : g1 - g0], func=RELU, bias=relu_bias[:])
+                    at += b - a
+                dst_cols = h[t][:, group[0][0] : group[-1][1]]
+                src_cols = acc[:, :at]
+                if t == 0 and g == 3:
+                    nc.vector.tensor_scalar_max(dst_cols, src_cols, 0.0)
                 else:
-                    nc.scalar.activation(out=h[t][:, g0:g1], in_=acc[:, : g1 - g0], func=RELU)
+                    nc.scalar.activation(out=dst_cols, in_=src_cols, func=RELU)
 
         def fetch(dst_tile, t, list_sb, v0, v1):
             nc.vector.tensor_copy(dst_tile[:, :, t, :], h[t][:].indirect(list_sb[:, v0 // 16 : v1 // 16]))

@@ -56,7 +56,7 @@ def tile_picked_zsgn_max_p_kernel(
 
         nc.sync.dma_start(offs_sb[:], offs)
         w1_rows = w1.rearrange("(p j) c -> p j c", j=PACK)
-        w1_parts = [(0, 128), (128, 256), (256, 384), (384, 512)]
+        w1_parts = [(0, 128), (128, 384), (384, 512)]
         w1_raw = [
             keep.tile([P, PACK, b - a], F32, name="w1_raw%d" % u, tag="w1_raw%d" % u, align_bytes=64)
             for u, (a, b) in enumerate(w1_parts)
@@ -66,7 +66,7 @@ def tile_picked_zsgn_max_p_kernel(
         load_scale_rows(nc.sync, x_scale_table, x_scales[0])
         x_word_table = keep.tile([P, T], I32, name="x_word_table", align_bytes=64)
         nc.sync.dma_start(out=x_word_table[:], in_=x_words[0].rearrange("p n t -> p (n t)").bitcast(I32))
-        for u in range(1, 4):
+        for u in range(1, 3):
             nc.sync.dma_start(out=w1_raw[u][:], in_=w1_rows[:, :, w1_parts[u][0] : w1_parts[u][1]])
         nc.sync.dma_start(pos2_sb[:], pos2)
         nc.sync.dma_start(foe1_sb[:], foe1)
@@ -86,11 +86,11 @@ def tile_picked_zsgn_max_p_kernel(
 
         w1_bf = keep.tile([P, PACK * P * PACK], BF16, name="w1_bf", align_bytes=64)
         dst = w1_bf[:].rearrange("p (t m j) -> p m j t", t=PACK, j=PACK)
-        srcs = [w1_raw[u][:].rearrange("p j (m t) -> p m j t", t=PACK) for u in range(4)]
-        for u in range(3):
-            nc.scalar.copy(out=dst[:, 32 * u : 32 * (u + 1)], in_=srcs[u])
-        nc.scalar.activation(out=dst[:, 96:128, :, 0], in_=srcs[3][:, :, :, 0], func=IDENTITY, bias=relu_bias[:])
-        nc.scalar.copy(out=dst[:, 96:128, :, 1:4], in_=srcs[3][:, :, :, 1:4])
+        srcs = [w1_raw[u][:].rearrange("p j (m t) -> p m j t", t=PACK) for u in range(3)]
+        nc.scalar.copy(out=dst[:, 0:32], in_=srcs[0])
+        nc.scalar.copy(out=dst[:, 32:64], in_=srcs[1][:, 0:32])
+        nc.scalar.activation(out=dst[:, 96:128, :, 0], in_=srcs[2][:, :, :, 0], func=IDENTITY, bias=relu_bias[:])
+        nc.scalar.copy(out=dst[:, 96:128, :, 1:4], in_=srcs[2][:, :, :, 1:4])
         w1_codes = keep.tile([P, PACK, P], U32, name="w1_codes", align_bytes=64)
         w1_sc = keep.tile([P, PACK, P], U8, name="w1_sc", align_bytes=64)
 
@@ -104,6 +104,7 @@ def tile_picked_zsgn_max_p_kernel(
         x_window = x_word_table[:].bitcast(U32)
         x_first = keep.tile([P, 768], U32, name="x_first", align_bytes=64)
         nc.vector.tensor_copy(x_first[:], x_window.indirect(offs_sb[:, 0:48]))
+        nc.vector.tensor_copy(out=dst[:, 64:96], in_=srcs[1][:, 32:64])
         quantise_w1(0, 1)
         x_rest = keep.tile([P, 256], U32, name="x_rest", tag="held", align_bytes=64)
         nc.vector.tensor_copy(x_rest[:], x_window.indirect(offs_sb[:, 48:64]))

@@ -56,18 +56,18 @@ def tile_picked_zsgn_max_p_kernel(
 
         nc.sync.dma_start(offs_sb[:], offs)
         w1_rows = w1.rearrange("(p j) c -> p j c", j=PACK)
-        w1_parts = [(0, 128), (128, 384), (384, 512)]
+        w1_parts = [(0, 384), (384, 512)]
         w1_raw = [
             keep.tile([P, PACK, b - a], F32, name="w1_raw%d" % u, tag="w1_raw%d" % u, align_bytes=64)
             for u, (a, b) in enumerate(w1_parts)
         ]
-        nc.sync.dma_start(out=w1_raw[0][:], in_=w1_rows[:, :, 0:128])
+        nc.sync.dma_start(out=w1_raw[0][:, 0, :], in_=w1_rows[:, 0, 0:384])
         nc.sync.dma_start(pos1_sb[:], pos1)
         load_scale_rows(nc.sync, x_scale_table, x_scales[0])
         x_word_table = keep.tile([P, T], I32, name="x_word_table", align_bytes=64)
         nc.sync.dma_start(out=x_word_table[:], in_=x_words[0].rearrange("p n t -> p (n t)").bitcast(I32))
-        for u in range(1, 3):
-            nc.sync.dma_start(out=w1_raw[u][:], in_=w1_rows[:, :, w1_parts[u][0] : w1_parts[u][1]])
+        nc.sync.dma_start(out=w1_raw[0][:, 1:4, :], in_=w1_rows[:, 1:4, 0:384])
+        nc.sync.dma_start(out=w1_raw[1][:], in_=w1_rows[:, :, 384:512])
         nc.sync.dma_start(pos2_sb[:], pos2)
         nc.sync.dma_start(foe1_sb[:], foe1)
         nc.sync.dma_start(foe2_sb[:], foe2)
@@ -86,11 +86,10 @@ def tile_picked_zsgn_max_p_kernel(
 
         w1_bf = keep.tile([P, PACK * P * PACK], BF16, name="w1_bf", align_bytes=64)
         dst = w1_bf[:].rearrange("p (t m j) -> p m j t", t=PACK, j=PACK)
-        srcs = [w1_raw[u][:].rearrange("p j (m t) -> p m j t", t=PACK) for u in range(3)]
-        nc.scalar.copy(out=dst[:, 0:32], in_=srcs[0])
-        nc.scalar.copy(out=dst[:, 32:64], in_=srcs[1][:, 0:32])
-        nc.scalar.activation(out=dst[:, 96:128, :, 0], in_=srcs[2][:, :, :, 0], func=IDENTITY, bias=relu_bias[:])
-        nc.scalar.copy(out=dst[:, 96:128, :, 1:4], in_=srcs[2][:, :, :, 1:4])
+        srcs = [w1_raw[u][:].rearrange("p j (m t) -> p m j t", t=PACK) for u in range(2)]
+        nc.scalar.copy(out=dst[:, 0:48], in_=srcs[0][:, 0:48])
+        nc.scalar.activation(out=dst[:, 96:128, :, 0], in_=srcs[1][:, :, :, 0], func=IDENTITY, bias=relu_bias[:])
+        nc.scalar.copy(out=dst[:, 96:128, :, 1:4], in_=srcs[1][:, :, :, 1:4])
         w1_codes = keep.tile([P, PACK, P], U32, name="w1_codes", align_bytes=64)
         w1_sc = keep.tile([P, PACK, P], U8, name="w1_sc", align_bytes=64)
 
@@ -104,7 +103,7 @@ def tile_picked_zsgn_max_p_kernel(
         x_window = x_word_table[:].bitcast(U32)
         x_first = keep.tile([P, 768], U32, name="x_first", align_bytes=64)
         nc.vector.tensor_copy(x_first[:], x_window.indirect(offs_sb[:, 0:48]))
-        nc.vector.tensor_copy(out=dst[:, 64:96], in_=srcs[1][:, 32:64])
+        nc.vector.tensor_copy(out=dst[:, 48:96], in_=srcs[0][:, 48:96])
         quantise_w1(0, 1)
         x_rest = keep.tile([P, 256], U32, name="x_rest", tag="held", align_bytes=64)
         nc.vector.tensor_copy(x_rest[:], x_window.indirect(offs_sb[:, 48:64]))

@@ -47,12 +47,12 @@ def tile_picked_zsgn_max_p_kernel(
         foe1_sb = lists.tile([P, V // 16], U16, name="foe1_sb")
         foe2_sb = lists.tile([P, V // 16], U16, name="foe2_sb")
 
-        x_scale_table = keep.tile([P, T], U8, name="x_scale_table", align_bytes=64)
+        x_scale_table = keep.tile([P, T], U8, name="x_scale_table", tag="scale_table", align_bytes=64)
         nc.vector.memset(x_scale_table[:].bitcast(I32), 0)
         zero = keep.tile([P, 1], F32, name="zero")
         nc.vector.memset(zero[:], 0.0)
-        w23_scales = keep.tile([P, 2, N], U8, name="w23_scales", align_bytes=64)
-        nc.vector.memset(w23_scales[:].rearrange("p a n -> p (a n)").bitcast(I32), 0)
+        x_sc = keep.tile([P, S], U8, name="x_sc", align_bytes=64)
+        nc.vector.memset(x_sc[:].bitcast(I32), 0)
 
         nc.sync.dma_start(offs_sb[:], offs)
         w1_rows = w1.rearrange("(p j) c -> p j c", j=PACK)
@@ -63,26 +63,33 @@ def tile_picked_zsgn_max_p_kernel(
         ]
         nc.sync.dma_start(out=w1_raw[0][:, 0, :], in_=w1_rows[:, 0, 0:384])
         nc.sync.dma_start(pos1_sb[:], pos1)
-        load_scale_rows(nc.sync, x_scale_table, x_scales[0])
+        nc.sync.dma_start(pos2_sb[:], pos2)
+        nc.sync.dma_start(out=x_scale_table[0:P:8, :].bitcast(I32), in_=x_scales[0].bitcast(I32))
         x_word_table = keep.tile([P, T], I32, name="x_word_table", align_bytes=64)
         nc.sync.dma_start(out=x_word_table[:], in_=x_words[0].rearrange("p n t -> p (n t)").bitcast(I32))
-        nc.sync.dma_start(out=w1_raw[0][:, 1:4, :], in_=w1_rows[:, 1:4, 0:384])
-        nc.sync.dma_start(out=w1_raw[1][:], in_=w1_rows[:, :, 384:512])
-        nc.sync.dma_start(pos2_sb[:], pos2)
         nc.sync.dma_start(foe1_sb[:], foe1)
         nc.sync.dma_start(foe2_sb[:], foe2)
-        w2_codes = keep.tile([P, 2 * N], U8, name="w2_codes", align_bytes=64)
-        w3_codes = keep.tile([P, 2 * N], U8, name="w3_codes", align_bytes=64)
-        nc.sync.dma_start(out=w2_codes[:].bitcast(I32), in_=w2_words[0].bitcast(I32))
-        nc.sync.dma_start(out=w3_codes[:].bitcast(I32), in_=w3_words[0].bitcast(I32))
-        load_scale_rows(nc.sync, w23_scales[:, 0, :], w2_scales[0])
-        load_scale_rows(nc.sync, w23_scales[:, 1, :], w3_scales[0])
+        nc.sync.dma_start(out=w1_raw[0][:, 1:4, :], in_=w1_rows[:, 1:4, 0:384])
+        nc.sync.dma_start(out=w1_raw[1][:], in_=w1_rows[:, :, 384:512])
 
         relu_bias = keep.tile([P, 1], F32, name="relu_bias", tag="held", align_bytes=64)
         nc.scalar.activation(out=relu_bias[:], in_=zero[:], func=TANH)
 
-        x_sc = keep.tile([P, S], U8, name="x_sc", align_bytes=64)
-        nc.vector.tensor_copy(x_sc[:], x_scale_table[:].indirect(offs_sb[:]))
+        x_sc_spread = keep.tile([P, S], U8, name="x_sc_spread", tag="spread", align_bytes=64)
+        nc.vector.tensor_copy(x_sc_spread[:], x_scale_table[:].indirect(offs_sb[:]))
+        for q in range(4):
+            nc.sync.dma_start(
+                out=x_sc[32 * q : 32 * q + 4, :].bitcast(I32), in_=x_sc_spread[32 * q : 32 * q + 32 : 8, :].bitcast(I32)
+            )
+        w23_codes = keep.tile([P, 2, 2 * N], U8, name="w23_codes", tag="scale_table", align_bytes=64)
+        w2_codes = w23_codes[:, 0, :]
+        w3_codes = w23_codes[:, 1, :]
+        nc.sync.dma_start(out=w2_codes.bitcast(I32), in_=w2_words[0].bitcast(I32))
+        nc.sync.dma_start(out=w3_codes.bitcast(I32), in_=w3_words[0].bitcast(I32))
+        w23_scales = keep.tile([P, 2, N], U8, name="w23_scales", tag="spread", align_bytes=64)
+        nc.vector.memset(w23_scales[:].rearrange("p a n -> p (a n)").bitcast(I32), 0)
+        load_scale_rows(nc.sync, w23_scales[:, 0, :], w2_scales[0])
+        load_scale_rows(nc.sync, w23_scales[:, 1, :], w3_scales[0])
 
         w1_bf = keep.tile([P, PACK * P * PACK], BF16, name="w1_bf", align_bytes=64)
         dst = w1_bf[:].rearrange("p (t m j) -> p m j t", t=PACK, j=PACK)

@@ -67,10 +67,10 @@ def tile_picked_zsgn_max_p_kernel(
         nc.sync.dma_start(out=x_scale_table[0:P:8, :].bitcast(I32), in_=x_scales[0].bitcast(I32))
         x_word_table = keep.tile([P, T], I32, name="x_word_table", align_bytes=64)
         nc.sync.dma_start(out=x_word_table[:], in_=x_words[0].rearrange("p n t -> p (n t)").bitcast(I32))
-        nc.sync.dma_start(foe1_sb[:], foe1)
-        nc.sync.dma_start(foe2_sb[:], foe2)
         nc.sync.dma_start(out=w1_raw[0][:, 1:4, :], in_=w1_rows[:, 1:4, 0:384])
         nc.sync.dma_start(out=w1_raw[1][:], in_=w1_rows[:, :, 384:512])
+        nc.sync.dma_start(foe1_sb[:], foe1)
+        nc.sync.dma_start(foe2_sb[:], foe2)
 
         relu_bias = keep.tile([P, 1], F32, name="relu_bias", tag="held", align_bytes=64)
         nc.scalar.activation(out=relu_bias[:], in_=zero[:], func=TANH)
@@ -78,7 +78,7 @@ def tile_picked_zsgn_max_p_kernel(
         x_sc_spread = keep.tile([P, S], U8, name="x_sc_spread", tag="spread", align_bytes=64)
         nc.vector.tensor_copy(x_sc_spread[:], x_scale_table[:].indirect(offs_sb[:]))
         for q in range(4):
-            nc.sync.dma_start(
+            nc.scalar.dma_start(
                 out=x_sc[32 * q : 32 * q + 4, :].bitcast(I32), in_=x_sc_spread[32 * q : 32 * q + 32 : 8, :].bitcast(I32)
             )
         w23_codes = keep.tile([P, 2, 2 * N], U8, name="w23_codes", tag="scale_table", align_bytes=64)

@@ -54,7 +54,6 @@ def tile_picked_zsgn_max_p_kernel(
         x_sc = keep.tile([P, S], U8, name="x_sc", align_bytes=64)
         nc.vector.memset(x_sc[:].bitcast(I32), 0)
 
-        nc.sync.dma_start(offs_sb[:], offs)
         w1_rows = w1.rearrange("(p j) c -> p j c", j=PACK)
         w1_parts = [(0, 384), (384, 512)]
         w1_raw = [
@@ -62,6 +61,7 @@ def tile_picked_zsgn_max_p_kernel(
             for u, (a, b) in enumerate(w1_parts)
         ]
         nc.sync.dma_start(out=w1_raw[0][:, 0, :], in_=w1_rows[:, 0, 0:384])
+        nc.sync.dma_start(offs_sb[:], offs)
         nc.sync.dma_start(pos1_sb[:], pos1)
         nc.sync.dma_start(pos2_sb[:], pos2)
         nc.sync.dma_start(out=x_scale_table[0:P:8, :].bitcast(I32), in_=x_scales[0].bitcast(I32))
@@ -75,7 +75,7 @@ def tile_picked_zsgn_max_p_kernel(
         relu_bias = keep.tile([P, 1], F32, name="relu_bias", tag="held", align_bytes=64)
         nc.scalar.activation(out=relu_bias[:], in_=zero[:], func=TANH)
 
-        x_sc_spread = keep.tile([P, S], U8, name="x_sc_spread", tag="spread", align_bytes=64)
+        x_sc_spread = keep.tile([P, S], U8, name="x_sc_spread", align_bytes=64)
         nc.vector.tensor_copy(x_sc_spread[:], x_scale_table[:].indirect(offs_sb[:]))
         for q in range(4):
             nc.scalar.dma_start(
@@ -86,10 +86,6 @@ def tile_picked_zsgn_max_p_kernel(
         w3_codes = w23_codes[:, 1, :]
         nc.sync.dma_start(out=w2_codes.bitcast(I32), in_=w2_words[0].bitcast(I32))
         nc.sync.dma_start(out=w3_codes.bitcast(I32), in_=w3_words[0].bitcast(I32))
-        w23_scales = keep.tile([P, 2, N], U8, name="w23_scales", tag="spread", align_bytes=64)
-        nc.vector.memset(w23_scales[:].rearrange("p a n -> p (a n)").bitcast(I32), 0)
-        load_scale_rows(nc.sync, w23_scales[:, 0, :], w2_scales[0])
-        load_scale_rows(nc.sync, w23_scales[:, 1, :], w3_scales[0])
 
         w1_bf = keep.tile([P, PACK * P * PACK], BF16, name="w1_bf", align_bytes=64)
         dst = w1_bf[:].rearrange("p (t m j) -> p m j t", t=PACK, j=PACK)
@@ -142,7 +138,7 @@ def tile_picked_zsgn_max_p_kernel(
                     at += b - a
                 dst_cols = h[t][:, group[0][0] : group[-1][1]]
                 src_cols = acc[:, :at]
-                if t == 0 and g == 3:
+                if t == 0 and g == 2:
                     nc.vector.tensor_scalar_max(dst_cols, src_cols, 0.0)
                 else:
                     nc.scalar.activation(out=dst_cols, in_=src_cols, func=RELU)
@@ -208,6 +204,11 @@ def tile_picked_zsgn_max_p_kernel(
                 larger_end(*pending)
                 pending = None
         larger_end(*pending)
+        w23_scales = keep.tile([P, 2, N], U8, name="w23_scales", tag="late_0", align_bytes=64)
+        nc.gpsimd.memset(w23_scales[:].rearrange("p a n -> p (a n)").bitcast(I32), 0)
+        load_scale_rows(nc.sync, w23_scales[:, 0, :], w2_scales[0])
+        load_scale_rows(nc.sync, w23_scales[:, 1, :], w3_scales[0])
+
         zp_woven = keep.tile([P, V, PACK], BF16, name="zp_woven", tag="late_c", align_bytes=64)
         for v0 in (0, half):
             weave(nc.scalar.copy, zp_woven[:, v0 : v0 + half, :], zp[:, :, v0 : v0 + half])

@@ -49,7 +49,7 @@ def tile_picked_zsgn_max_p_kernel(
 
         x_scale_table = keep.tile([P, T], U8, name="x_scale_table", tag="scale_table", align_bytes=64)
         nc.vector.memset(x_scale_table[:].bitcast(I32), 0)
-        zero = keep.tile([P, 1], F32, name="zero")
+        zero = keep.tile([P, 1], F32, name="zero", tag="foes_first", align_bytes=64)
         nc.vector.memset(zero[:], 0.0)
         x_sc = keep.tile([P, S], U8, name="x_sc", align_bytes=64)
         nc.vector.memset(x_sc[:].bitcast(I32), 0)
@@ -140,6 +140,8 @@ def tile_picked_zsgn_max_p_kernel(
                 src_cols = acc[:, :at]
                 if t == 0 and g == 2:
                     nc.vector.tensor_scalar_max(dst_cols, src_cols, 0.0)
+                elif t == PACK - 1 and g == 1:
+                    nc.scalar.activation(out=dst_cols, in_=src_cols, func=RELU, bias=zero[:])
                 else:
                     nc.scalar.activation(out=dst_cols, in_=src_cols, func=RELU)
 
@@ -178,7 +180,7 @@ def tile_picked_zsgn_max_p_kernel(
 
         head = V - CHUNK
         half = V // 2
-        zp = keep.tile([P, PACK, V], BF16, name="zp", tag="late_d", align_bytes=64)
+        zp_woven = keep.tile([P, V, PACK], BF16, name="zp_woven", align_bytes=64)
         def larger_begin(name, first, second, tag):
             diff = keep.tile([P, V], F32, name="diff" + name, tag=tag, align_bytes=64)
             nc.gpsimd.tensor_tensor(diff[:], first, second, SUB)
@@ -199,7 +201,7 @@ def tile_picked_zsgn_max_p_kernel(
             diff = larger_begin("%d" % t, friend1[:], friend2[:], diff_slots[t])
             if pending is not None:
                 larger_end(*pending)
-            pending = ("%d" % t, diff, friend2[:], zp[:, t, :])
+            pending = ("%d" % t, diff, friend2[:], zp_woven[:, :, t])
             if t == 0:
                 larger_end(*pending)
                 pending = None
@@ -209,13 +211,9 @@ def tile_picked_zsgn_max_p_kernel(
         load_scale_rows(nc.sync, w23_scales[:, 0, :], w2_scales[0])
         load_scale_rows(nc.sync, w23_scales[:, 1, :], w3_scales[0])
 
-        zp_woven = keep.tile([P, V, PACK], BF16, name="zp_woven", tag="late_c", align_bytes=64)
-        for v0 in (0, half):
-            weave(nc.scalar.copy, zp_woven[:, v0 : v0 + half, :], zp[:, :, v0 : v0 + half])
-
         last = PACK - 1
         tail = CHUNKS - 1
-        foes1 = keep.tile([P, CHUNKS, PACK, CHUNK], BF16, name="foes1", tag="late_2", align_bytes=64)
+        foes1 = keep.tile([P, CHUNKS, PACK, CHUNK], BF16, name="foes1", tag="foes_first", align_bytes=64)
         foes2 = keep.tile([P, CHUNKS, PACK, CHUNK], BF16, name="foes2", tag="late_3", align_bytes=64)
         for t in range(PACK):
             fetch(foes1, t, foe1_sb, 0, V)
@@ -228,7 +226,7 @@ def tile_picked_zsgn_max_p_kernel(
         quantise(zp_codes, zp_sc, zp_woven, 0, half)
         for c in range(CHUNKS // 2):
             product(0, zp_codes, zp_sc, c)
-        zn = keep.tile([P, CHUNKS + 1, PACK * CHUNK], BF16, name="zn", tag="late_d", align_bytes=64)
+        zn = keep.tile([P, CHUNKS + 1, PACK * CHUNK], BF16, name="zn", tag="excess3", align_bytes=64)
         tail2 = zn[:, tail, :].rearrange("p (v t) -> p v t", t=PACK)
         tail1 = zn[:, tail + 1, :].rearrange("p (v t) -> p v t", t=PACK)
         weave(nc.scalar.copy, tail1, foes1[:, tail])

@@ -41,23 +41,23 @@ def tile_picked_zsgn_max_p_kernel(
         keep = ctx.enter_context(tc.tile_pool(name="keep", bufs=1))
         psum = ctx.enter_context(tc.psum_pool(name="psum", bufs=1))
 
-        offs_sb = lists.tile([P, S // 16], U16, name="offs_sb")
-        pos1_sb = lists.tile([P, V // 16], U16, name="pos1_sb")
-        pos2_sb = lists.tile([P, V // 16], U16, name="pos2_sb")
-        foe1_sb = lists.tile([P, V // 16], U16, name="foe1_sb")
-        foe2_sb = lists.tile([P, V // 16], U16, name="foe2_sb")
+        offs_sb = lists.tile([P, S // 16], U16, name="offs_sb", align_bytes=256)
+        pos1_sb = lists.tile([P, V // 16], U16, name="pos1_sb", align_bytes=256)
+        pos2_sb = lists.tile([P, V // 16], U16, name="pos2_sb", align_bytes=256)
+        foe1_sb = lists.tile([P, V // 16], U16, name="foe1_sb", align_bytes=256)
+        foe2_sb = lists.tile([P, V // 16], U16, name="foe2_sb", align_bytes=256)
 
-        x_scale_table = keep.tile([P, T], U8, name="x_scale_table", tag="scale_table", align_bytes=64)
+        x_scale_table = keep.tile([P, T], U8, name="x_scale_table", tag="scale_table", align_bytes=256)
         nc.vector.memset(x_scale_table[:].bitcast(I32), 0)
-        zero = keep.tile([P, 1], F32, name="zero", tag="foes_first", align_bytes=64)
+        zero = keep.tile([P, 1], F32, name="zero", tag="foes_first", align_bytes=256)
         nc.vector.memset(zero[:], 0.0)
-        x_sc = keep.tile([P, S], U8, name="x_sc", align_bytes=64)
+        x_sc = keep.tile([P, S], U8, name="x_sc", align_bytes=256)
         nc.vector.memset(x_sc[:].bitcast(I32), 0)
 
         w1_rows = w1.rearrange("(p j) c -> p j c", j=PACK)
         w1_parts = [(0, 384), (384, 512)]
         w1_raw = [
-            keep.tile([P, PACK, b - a], F32, name="w1_raw%d" % u, tag="w1_raw%d" % u, align_bytes=64)
+            keep.tile([P, PACK, b - a], F32, name="w1_raw%d" % u, tag="w1_raw%d" % u, align_bytes=256)
             for u, (a, b) in enumerate(w1_parts)
         ]
         nc.sync.dma_start(out=w1_raw[0][:, 0, :], in_=w1_rows[:, 0, 0:384])
@@ -65,36 +65,36 @@ def tile_picked_zsgn_max_p_kernel(
         nc.sync.dma_start(pos1_sb[:], pos1)
         nc.sync.dma_start(pos2_sb[:], pos2)
         nc.sync.dma_start(out=x_scale_table[0:P:8, :].bitcast(I32), in_=x_scales[0].bitcast(I32))
-        x_word_table = keep.tile([P, T], I32, name="x_word_table", align_bytes=64)
+        x_word_table = keep.tile([P, T], I32, name="x_word_table", align_bytes=256)
         nc.sync.dma_start(out=x_word_table[:], in_=x_words[0].rearrange("p n t -> p (n t)").bitcast(I32))
         nc.sync.dma_start(out=w1_raw[0][:, 1:4, :], in_=w1_rows[:, 1:4, 0:384])
         nc.sync.dma_start(out=w1_raw[1][:], in_=w1_rows[:, :, 384:512])
         nc.sync.dma_start(foe1_sb[:], foe1)
         nc.sync.dma_start(foe2_sb[:], foe2)
 
-        relu_bias = keep.tile([P, 1], F32, name="relu_bias", tag="held", align_bytes=64)
+        relu_bias = keep.tile([P, 1], F32, name="relu_bias", tag="held", align_bytes=256)
         nc.scalar.activation(out=relu_bias[:], in_=zero[:], func=TANH)
 
-        x_sc_spread = keep.tile([P, S], U8, name="x_sc_spread", align_bytes=64)
+        x_sc_spread = keep.tile([P, S], U8, name="x_sc_spread", align_bytes=256)
         nc.vector.tensor_copy(x_sc_spread[:], x_scale_table[:].indirect(offs_sb[:]))
         for q in range(4):
             nc.scalar.dma_start(
                 out=x_sc[32 * q : 32 * q + 4, :].bitcast(I32), in_=x_sc_spread[32 * q : 32 * q + 32 : 8, :].bitcast(I32)
             )
-        w23_codes = keep.tile([P, 2, 2 * N], U8, name="w23_codes", tag="scale_table", align_bytes=64)
+        w23_codes = keep.tile([P, 2, 2 * N], U8, name="w23_codes", tag="scale_table", align_bytes=256)
         w2_codes = w23_codes[:, 0, :]
         w3_codes = w23_codes[:, 1, :]
         nc.sync.dma_start(out=w2_codes.bitcast(I32), in_=w2_words[0].bitcast(I32))
         nc.sync.dma_start(out=w3_codes.bitcast(I32), in_=w3_words[0].bitcast(I32))
 
-        w1_bf = keep.tile([P, PACK * P * PACK], BF16, name="w1_bf", align_bytes=64)
+        w1_bf = keep.tile([P, PACK * P * PACK], BF16, name="w1_bf", align_bytes=256)
         dst = w1_bf[:].rearrange("p (t m j) -> p m j t", t=PACK, j=PACK)
         srcs = [w1_raw[u][:].rearrange("p j (m t) -> p m j t", t=PACK) for u in range(2)]
         nc.scalar.copy(out=dst[:, 0:48], in_=srcs[0][:, 0:48])
         nc.scalar.activation(out=dst[:, 96:128, :, 0], in_=srcs[1][:, :, :, 0], func=IDENTITY, bias=relu_bias[:])
         nc.scalar.copy(out=dst[:, 96:128, :, 1:4], in_=srcs[1][:, :, :, 1:4])
-        w1_codes = keep.tile([P, PACK, P], U32, name="w1_codes", align_bytes=64)
-        w1_sc = keep.tile([P, PACK, P], U8, name="w1_sc", align_bytes=64)
+        w1_codes = keep.tile([P, PACK, P], U32, name="w1_codes", align_bytes=256)
+        w1_sc = keep.tile([P, PACK, P], U8, name="w1_sc", align_bytes=256)
 
         def quantise_w1(t0, t1):
             nc.vector.quantize_mx(
@@ -104,11 +104,11 @@ def tile_picked_zsgn_max_p_kernel(
             )
 
         x_window = x_word_table[:].bitcast(U32)
-        x_first = keep.tile([P, 768], U32, name="x_first", align_bytes=64)
+        x_first = keep.tile([P, 768], U32, name="x_first", align_bytes=256)
         nc.vector.tensor_copy(x_first[:], x_window.indirect(offs_sb[:, 0:48]))
         nc.vector.tensor_copy(out=dst[:, 48:96], in_=srcs[0][:, 48:96])
         quantise_w1(0, 1)
-        x_rest = keep.tile([P, 256], U32, name="x_rest", tag="held", align_bytes=64)
+        x_rest = keep.tile([P, 256], U32, name="x_rest", tag="held", align_bytes=256)
         nc.vector.tensor_copy(x_rest[:], x_window.indirect(offs_sb[:, 48:64]))
         quantise_w1(1, 2)
         quantise_w1(2, 4)
@@ -116,7 +116,7 @@ def tile_picked_zsgn_max_p_kernel(
         def picked(a, b):
             return x_first[:, a:b] if b <= 768 else x_rest[:, a - 768 : b - 768]
 
-        h = [keep.tile([P, S], F32, name="h%d" % t, align_bytes=64) for t in range(PACK)]
+        h = [keep.tile([P, S], F32, name="h%d" % t, align_bytes=256) for t in range(PACK)]
         bank = 0
         first_groups = [[(0, 256)], [(256, 512)], [(512, 768)], [(768, 896)], [(896, 1024)]]
         later_groups = [[(0, 512)], [(512, 768), (768, 1024)]]
@@ -180,22 +180,22 @@ def tile_picked_zsgn_max_p_kernel(
 
         head = V - CHUNK
         half = V // 2
-        zp_woven = keep.tile([P, V, PACK], BF16, name="zp_woven", align_bytes=64)
+        zp_woven = keep.tile([P, V, PACK], BF16, name="zp_woven", align_bytes=256)
         def larger_begin(name, first, second, tag):
-            diff = keep.tile([P, V], F32, name="diff" + name, tag=tag, align_bytes=64)
+            diff = keep.tile([P, V], F32, name="diff" + name, tag=tag, align_bytes=256)
             nc.gpsimd.tensor_tensor(diff[:], first, second, SUB)
             return diff
 
         def larger_end(name, diff, second, dst_plane):
-            excess = keep.tile([P, V], F32, name="excess" + name, tag="excess" + name, align_bytes=64)
+            excess = keep.tile([P, V], F32, name="excess" + name, tag="excess" + name, align_bytes=256)
             nc.scalar.activation(out=excess[:], in_=diff[:], func=RELU)
             nc.gpsimd.tensor_tensor(dst_plane, excess[:], second, ADD)
 
         diff_slots = ["diff0", "excess0", "late_1", "excess1"]
         pending = None
         for t in range(PACK):
-            friend1 = keep.tile([P, V], F32, name="friend1_%d" % t, tag="late_%d" % t, align_bytes=64)
-            friend2 = keep.tile([P, V], F32, name="friend2_%d" % t, align_bytes=64)
+            friend1 = keep.tile([P, V], F32, name="friend1_%d" % t, tag="late_%d" % t, align_bytes=256)
+            friend2 = keep.tile([P, V], F32, name="friend2_%d" % t, align_bytes=256)
             nc.vector.tensor_copy(friend1[:], h[t][:].indirect(pos1_sb[:]))
             nc.vector.tensor_copy(friend2[:], h[t][:].indirect(pos2_sb[:]))
             diff = larger_begin("%d" % t, friend1[:], friend2[:], diff_slots[t])
@@ -206,34 +206,34 @@ def tile_picked_zsgn_max_p_kernel(
                 larger_end(*pending)
                 pending = None
         larger_end(*pending)
-        w23_scales = keep.tile([P, 2, N], U8, name="w23_scales", tag="late_0", align_bytes=64)
+        w23_scales = keep.tile([P, 2, N], U8, name="w23_scales", tag="late_0", align_bytes=256)
         nc.gpsimd.memset(w23_scales[:].rearrange("p a n -> p (a n)").bitcast(I32), 0)
         load_scale_rows(nc.sync, w23_scales[:, 0, :], w2_scales[0])
         load_scale_rows(nc.sync, w23_scales[:, 1, :], w3_scales[0])
 
         last = PACK - 1
         tail = CHUNKS - 1
-        foes1 = keep.tile([P, CHUNKS, PACK, CHUNK], BF16, name="foes1", tag="foes_first", align_bytes=64)
-        foes2 = keep.tile([P, CHUNKS, PACK, CHUNK], BF16, name="foes2", tag="late_3", align_bytes=64)
+        foes1 = keep.tile([P, CHUNKS, PACK, CHUNK], BF16, name="foes1", tag="foes_first", align_bytes=256)
+        foes2 = keep.tile([P, CHUNKS, PACK, CHUNK], BF16, name="foes2", tag="late_3", align_bytes=256)
         for t in range(PACK):
             fetch(foes1, t, foe1_sb, 0, V)
         for t in range(last):
             fetch(foes2, t, foe2_sb, 0, V)
         fetch(foes2[:, :tail], last, foe2_sb, 0, head)
         nc.scalar.copy(out=foes2[:, tail, last, :], in_=foes1[:, tail, last, :])
-        zp_codes = keep.tile([P, V], U32, name="zp_codes", align_bytes=64)
-        zp_sc = keep.tile([P, V], U8, name="zp_sc", align_bytes=64)
+        zp_codes = keep.tile([P, V], U32, name="zp_codes", align_bytes=256)
+        zp_sc = keep.tile([P, V], U8, name="zp_sc", align_bytes=256)
         quantise(zp_codes, zp_sc, zp_woven, 0, half)
         for c in range(CHUNKS // 2):
             product(0, zp_codes, zp_sc, c)
-        zn = keep.tile([P, CHUNKS + 1, PACK * CHUNK], BF16, name="zn", tag="excess3", align_bytes=64)
+        zn = keep.tile([P, CHUNKS + 1, PACK * CHUNK], BF16, name="zn", tag="excess3", align_bytes=256)
         tail2 = zn[:, tail, :].rearrange("p (v t) -> p v t", t=PACK)
         tail1 = zn[:, tail + 1, :].rearrange("p (v t) -> p v t", t=PACK)
         weave(nc.scalar.copy, tail1, foes1[:, tail])
         weave(nc.scalar.copy, tail2, foes2[:, tail])
-        zn_woven = keep.tile([P, head, PACK], BF16, name="zn_woven", align_bytes=64)
-        zn_codes = keep.tile([P, V], U32, name="zn_codes", align_bytes=64)
-        zn_sc = keep.tile([P, V], U8, name="zn_sc", align_bytes=64)
+        zn_woven = keep.tile([P, head, PACK], BF16, name="zn_woven", align_bytes=256)
+        zn_codes = keep.tile([P, V], U32, name="zn_codes", align_bytes=256)
+        zn_sc = keep.tile([P, V], U8, name="zn_sc", align_bytes=256)
 
         def larger_foes(c):
             planes = zn[:, c, :].rearrange("p (t v) -> p t v", t=PACK)
@@ -253,7 +253,7 @@ def tile_picked_zsgn_max_p_kernel(
         quantise(zn_codes, zn_sc, zn_woven, 2 * CHUNK, head)
         nc.vector.quantize_mx(out=zn_codes[:, head:].bitcast(FP8X4), scales=zn_sc[:, head:], in_=zn[:, 1, :])
 
-        res = keep.tile([P, N // P, V], F32, name="res", align_bytes=64)
+        res = keep.tile([P, N // P, V], F32, name="res", align_bytes=256)
         out_v = out.rearrange("(b p) v -> p b v", p=P)
         for c in range(CHUNKS):
             cols = slice(c * CHUNK, (c + 1) * CHUNK)

@@ -51,24 +51,22 @@ def tile_picked_zsgn_max_p_kernel(
         nc.vector.memset(x_scale_table[:].bitcast(I32), 0)
         zero = keep.tile([P, 1], F32, name="zero", tag="foes_first", align_bytes=256)
         nc.vector.memset(zero[:], 0.0)
+        cast_bias = keep.tile([P, 1], F32, name="cast_bias", tag="held_b", align_bytes=256)
+        nc.vector.memset(cast_bias[:], 0.0)
         x_sc = keep.tile([P, S], U8, name="x_sc", align_bytes=256)
         nc.vector.memset(x_sc[:].bitcast(I32), 0)
 
-        w1_rows = w1.rearrange("(p j) c -> p j c", j=PACK)
-        w1_parts = [(0, 384), (384, 512)]
-        w1_raw = [
-            keep.tile([P, PACK, b - a], F32, name="w1_raw%d" % u, tag="w1_raw%d" % u, align_bytes=256)
-            for u, (a, b) in enumerate(w1_parts)
-        ]
-        nc.sync.dma_start(out=w1_raw[0][:, 0, :], in_=w1_rows[:, 0, 0:384])
+        w1_flat = w1.rearrange("(p j) c -> p (j c)", j=PACK)
+        w1_raw = keep.tile([P, PACK * H], F32, name="w1_raw", align_bytes=256)
+        nc.sync.dma_start(out=w1_raw[:, 0:H], in_=w1_flat[:, 0:H])
         nc.sync.dma_start(offs_sb[:], offs)
         nc.sync.dma_start(pos1_sb[:], pos1)
         nc.sync.dma_start(pos2_sb[:], pos2)
         nc.sync.dma_start(out=x_scale_table[0:P:8, :].bitcast(I32), in_=x_scales[0].bitcast(I32))
+        nc.sync.dma_start(out=w1_raw[:, H : 2 * H], in_=w1_flat[:, H : 2 * H])
         x_word_table = keep.tile([P, T], I32, name="x_word_table", align_bytes=256)
         nc.sync.dma_start(out=x_word_table[:], in_=x_words[0].rearrange("p n t -> p (n t)").bitcast(I32))
-        nc.sync.dma_start(out=w1_raw[0][:, 1:4, :], in_=w1_rows[:, 1:4, 0:384])
-        nc.sync.dma_start(out=w1_raw[1][:], in_=w1_rows[:, :, 384:512])
+        nc.sync.dma_start(out=w1_raw[:, 2 * H :], in_=w1_flat[:, 2 * H :])
         nc.sync.dma_start(foe1_sb[:], foe1)
         nc.sync.dma_start(foe2_sb[:], foe2)
 
@@ -87,31 +85,33 @@ def tile_picked_zsgn_max_p_kernel(
         nc.sync.dma_start(out=w2_codes.bitcast(I32), in_=w2_words[0].bitcast(I32))
         nc.sync.dma_start(out=w3_codes.bitcast(I32), in_=w3_words[0].bitcast(I32))
 
-        w1_bf = keep.tile([P, PACK * P * PACK], BF16, name="w1_bf", align_bytes=256)
-        dst = w1_bf[:].rearrange("p (t m j) -> p m j t", t=PACK, j=PACK)
-        srcs = [w1_raw[u][:].rearrange("p j (m t) -> p m j t", t=PACK) for u in range(2)]
-        nc.scalar.copy(out=dst[:, 0:48], in_=srcs[0][:, 0:48])
-        nc.scalar.activation(out=dst[:, 96:128, :, 0], in_=srcs[1][:, :, :, 0], func=IDENTITY, bias=relu_bias[:])
-        nc.scalar.copy(out=dst[:, 96:128, :, 1:4], in_=srcs[1][:, :, :, 1:4])
+        src = w1_raw[:].rearrange("p (j m t) -> p m j t", j=PACK, t=PACK)
+        w1_bf_a = keep.tile([P, 2 * P * PACK], BF16, name="w1_bf_a", align_bytes=256)
+        dst_a = w1_bf_a[:].rearrange("p (t m j) -> p m j t", t=2, j=PACK)
+        nc.scalar.copy(out=dst_a[:, :, 0:2, :], in_=src[:, :, 0:2, 0:2])
+        nc.scalar.activation(out=dst_a[:, :, 2:4, 0], in_=src[:, :, 2:4, 0], func=IDENTITY, bias=relu_bias[:])
+        nc.scalar.activation(out=dst_a[:, :, 2:4, 1], in_=src[:, :, 2:4, 1], func=IDENTITY, bias=cast_bias[:])
         w1_codes = keep.tile([P, PACK, P], U32, name="w1_codes", align_bytes=256)
         w1_sc = keep.tile([P, PACK, P], U8, name="w1_sc", align_bytes=256)
 
-        def quantise_w1(t0, t1):
+        def quantise_w1(t0, t1, woven):
             nc.vector.quantize_mx(
                 out=w1_codes[:, t0:t1, :].rearrange("p t m -> p (t m)").bitcast(FP8X4),
                 scales=w1_sc[:, t0:t1, :].rearrange("p t m -> p (t m)"),
-                in_=w1_bf[:, t0 * P * PACK : t1 * P * PACK],
+                in_=woven,
             )
 
         x_window = x_word_table[:].bitcast(U32)
         x_first = keep.tile([P, 768], U32, name="x_first", align_bytes=256)
         nc.vector.tensor_copy(x_first[:], x_window.indirect(offs_sb[:, 0:48]))
-        nc.vector.tensor_copy(out=dst[:, 48:96], in_=srcs[0][:, 48:96])
-        quantise_w1(0, 1)
+        quantise_w1(0, 1, w1_bf_a[:, : P * PACK])
         x_rest = keep.tile([P, 256], U32, name="x_rest", tag="held", align_bytes=256)
         nc.vector.tensor_copy(x_rest[:], x_window.indirect(offs_sb[:, 48:64]))
-        quantise_w1(1, 2)
-        quantise_w1(2, 4)
+        w1_bf_b = keep.tile([P, 2 * P * PACK], BF16, name="w1_bf_b", tag="held_b", align_bytes=256)
+        dst_b = w1_bf_b[:].rearrange("p (t m j) -> p m j t", t=2, j=PACK)
+        nc.vector.tensor_copy(out=dst_b, in_=src[:, :, :, 2:4])
+        quantise_w1(1, 2, w1_bf_a[:, P * PACK :])
+        quantise_w1(2, 4, w1_bf_b[:])
 
         def picked(a, b):
             return x_first[:, a:b] if b <= 768 else x_rest[:, a - 768 : b - 768]
@@ -138,9 +138,7 @@ def tile_picked_zsgn_max_p_kernel(
                     at += b - a
                 dst_cols = h[t][:, group[0][0] : group[-1][1]]
                 src_cols = acc[:, :at]
-                if t == 0 and g == 2:
-                    nc.vector.tensor_scalar_max(dst_cols, src_cols, 0.0)
-                elif t == PACK - 1 and g == 1:
+                if t == PACK - 1 and g == 1:
                     nc.scalar.activation(out=dst_cols, in_=src_cols, func=RELU, bias=zero[:])
                 else:
                     nc.scalar.activation(out=dst_cols, in_=src_cols, func=RELU)

@@ -63,9 +63,9 @@ def tile_picked_zsgn_max_p_kernel(
         nc.sync.dma_start(pos1_sb[:], pos1)
         nc.sync.dma_start(pos2_sb[:], pos2)
         nc.sync.dma_start(out=x_scale_table[0:P:8, :].bitcast(I32), in_=x_scales[0].bitcast(I32))
-        nc.sync.dma_start(out=w1_raw[:, H : 2 * H], in_=w1_flat[:, H : 2 * H])
         x_word_table = keep.tile([P, T], I32, name="x_word_table", align_bytes=256)
         nc.sync.dma_start(out=x_word_table[:], in_=x_words[0].rearrange("p n t -> p (n t)").bitcast(I32))
+        nc.sync.dma_start(out=w1_raw[:, H : 2 * H], in_=w1_flat[:, H : 2 * H])
         nc.sync.dma_start(out=w1_raw[:, 2 * H :], in_=w1_flat[:, 2 * H :])
         nc.sync.dma_start(foe1_sb[:], foe1)
         nc.sync.dma_start(foe2_sb[:], foe2)
@@ -89,7 +89,7 @@ def tile_picked_zsgn_max_p_kernel(
         w1_bf_a = keep.tile([P, 2 * P * PACK], BF16, name="w1_bf_a", align_bytes=256)
         dst_a = w1_bf_a[:].rearrange("p (t m j) -> p m j t", t=2, j=PACK)
         nc.scalar.copy(out=dst_a[:, :, 0:2, :], in_=src[:, :, 0:2, 0:2])
-        nc.scalar.activation(out=dst_a[:, :, 2:4, 0], in_=src[:, :, 2:4, 0], func=IDENTITY, bias=relu_bias[:])
+        nc.scalar.activation(out=dst_a[:, 80:, 2:4, 0], in_=src[:, 80:, 2:4, 0], func=IDENTITY, bias=relu_bias[:])
         nc.scalar.activation(out=dst_a[:, :, 2:4, 1], in_=src[:, :, 2:4, 1], func=IDENTITY, bias=cast_bias[:])
         w1_codes = keep.tile([P, PACK, P], U32, name="w1_codes", align_bytes=256)
         w1_sc = keep.tile([P, PACK, P], U8, name="w1_sc", align_bytes=256)
@@ -104,6 +104,7 @@ def tile_picked_zsgn_max_p_kernel(
         x_window = x_word_table[:].bitcast(U32)
         x_first = keep.tile([P, 768], U32, name="x_first", align_bytes=256)
         nc.vector.tensor_copy(x_first[:], x_window.indirect(offs_sb[:, 0:48]))
+        nc.vector.tensor_copy(out=dst_a[:, :80, 2:4, 0], in_=src[:, :80, 2:4, 0])
         quantise_w1(0, 1, w1_bf_a[:, : P * PACK])
         x_rest = keep.tile([P, 256], U32, name="x_rest", tag="held", align_bytes=256)
         nc.vector.tensor_copy(x_rest[:], x_window.indirect(offs_sb[:, 48:64]))

@@ -51,8 +51,6 @@ def tile_picked_zsgn_max_p_kernel(
         nc.vector.memset(x_scale_table[:].bitcast(I32), 0)
         zero = keep.tile([P, 1], F32, name="zero", tag="foes_first", align_bytes=256)
         nc.vector.memset(zero[:], 0.0)
-        cast_bias = keep.tile([P, 1], F32, name="cast_bias", tag="held_b", align_bytes=256)
-        nc.vector.memset(cast_bias[:], 0.0)
         x_sc = keep.tile([P, S], U8, name="x_sc", align_bytes=256)
         nc.vector.memset(x_sc[:].bitcast(I32), 0)
 
@@ -61,12 +59,11 @@ def tile_picked_zsgn_max_p_kernel(
         nc.sync.dma_start(out=w1_raw[:, 0:H], in_=w1_flat[:, 0:H])
         nc.sync.dma_start(offs_sb[:], offs)
         nc.sync.dma_start(pos1_sb[:], pos1)
-        nc.sync.dma_start(pos2_sb[:], pos2)
         nc.sync.dma_start(out=x_scale_table[0:P:8, :].bitcast(I32), in_=x_scales[0].bitcast(I32))
         x_word_table = keep.tile([P, T], I32, name="x_word_table", align_bytes=256)
         nc.sync.dma_start(out=x_word_table[:], in_=x_words[0].rearrange("p n t -> p (n t)").bitcast(I32))
-        nc.sync.dma_start(out=w1_raw[:, H : 2 * H], in_=w1_flat[:, H : 2 * H])
-        nc.sync.dma_start(out=w1_raw[:, 2 * H :], in_=w1_flat[:, 2 * H :])
+        nc.sync.dma_start(out=w1_raw[:, H:], in_=w1_flat[:, H:])
+        nc.sync.dma_start(pos2_sb[:], pos2)
         nc.sync.dma_start(foe1_sb[:], foe1)
         nc.sync.dma_start(foe2_sb[:], foe2)
 
@@ -88,9 +85,10 @@ def tile_picked_zsgn_max_p_kernel(
         src = w1_raw[:].rearrange("p (j m t) -> p m j t", j=PACK, t=PACK)
         w1_bf_a = keep.tile([P, 2 * P * PACK], BF16, name="w1_bf_a", align_bytes=256)
         dst_a = w1_bf_a[:].rearrange("p (t m j) -> p m j t", t=2, j=PACK)
-        nc.scalar.copy(out=dst_a[:, :, 0:2, :], in_=src[:, :, 0:2, 0:2])
-        nc.scalar.activation(out=dst_a[:, 80:, 2:4, 0], in_=src[:, 80:, 2:4, 0], func=IDENTITY, bias=relu_bias[:])
-        nc.scalar.activation(out=dst_a[:, :, 2:4, 1], in_=src[:, :, 2:4, 1], func=IDENTITY, bias=cast_bias[:])
+        w1_bf_b = keep.tile([P, 2 * P * PACK], BF16, name="w1_bf_b", align_bytes=256)
+        dst_b = w1_bf_b[:].rearrange("p (t m j) -> p m j t", t=2, j=PACK)
+        nc.scalar.activation(out=dst_a[:, 86:], in_=src[:, 86:, :, 0:2], func=IDENTITY, bias=relu_bias[:])
+        nc.scalar.copy(out=dst_b[:, :88], in_=src[:, :88, :, 2:4])
         w1_codes = keep.tile([P, PACK, P], U32, name="w1_codes", align_bytes=256)
         w1_sc = keep.tile([P, PACK, P], U8, name="w1_sc", align_bytes=256)
 
@@ -104,13 +102,11 @@ def tile_picked_zsgn_max_p_kernel(
         x_window = x_word_table[:].bitcast(U32)
         x_first = keep.tile([P, 768], U32, name="x_first", align_bytes=256)
         nc.vector.tensor_copy(x_first[:], x_window.indirect(offs_sb[:, 0:48]))
-        nc.vector.tensor_copy(out=dst_a[:, :80, 2:4, 0], in_=src[:, :80, 2:4, 0])
+        nc.vector.tensor_copy(out=dst_a[:, :86], in_=src[:, :86, :, 0:2])
+        nc.vector.tensor_copy(out=dst_b[:, 88:], in_=src[:, 88:, :, 2:4])
         quantise_w1(0, 1, w1_bf_a[:, : P * PACK])
         x_rest = keep.tile([P, 256], U32, name="x_rest", tag="held", align_bytes=256)
         nc.vector.tensor_copy(x_rest[:], x_window.indirect(offs_sb[:, 48:64]))
-        w1_bf_b = keep.tile([P, 2 * P * PACK], BF16, name="w1_bf_b", tag="held_b", align_bytes=256)
-        dst_b = w1_bf_b[:].rearrange("p (t m j) -> p m j t", t=2, j=PACK)
-        nc.vector.tensor_copy(out=dst_b, in_=src[:, :, :, 2:4])
         quantise_w1(1, 2, w1_bf_a[:, P * PACK :])
         quantise_w1(2, 4, w1_bf_b[:])
 
@@ -139,7 +135,9 @@ def tile_picked_zsgn_max_p_kernel(
                     at += b - a
                 dst_cols = h[t][:, group[0][0] : group[-1][1]]
                 src_cols = acc[:, :at]
-                if t == PACK - 1 and g == 1:
+                if t == 0 and g == 2:
+                    nc.vector.tensor_scalar_max(dst_cols, src_cols, 0.0)
+                elif t == PACK - 1 and g == 1:
                     nc.scalar.activation(out=dst_cols, in_=src_cols, func=RELU, bias=zero[:])
                 else:
                     nc.scalar.activation(out=dst_cols, in_=src_cols, func=RELU)

@@ -257,7 +257,4 @@ def tile_picked_zsgn_max_p_kernel(
             product(1, zn_codes, zn_sc, c)
             for b in range(N // P):
                 nc.scalar.activation(out=res[:, b, cols], in_=accs[(b, c)][:, :CHUNK], func=TANH)
-                if c == tail:
-                    nc.sync.dma_start(out=out_v[:, b, cols], in_=res[:, b, cols])
-            if c != tail:
-                nc.sync.dma_start(out=out_v[:, :, cols], in_=res[:, :, cols])
+                nc.sync.dma_start(out=out_v[:, b, cols], in_=res[:, b, cols])

@@ -14,17 +14,15 @@ U8 = mybir.dt.uint8
 FP8X4 = mybir.dt.float8_e4m3fn_x4
 FP4X4 = mybir.dt.float4_e2m1fn_x4
 MAX = mybir.AluOpType.max
-ADD = mybir.AluOpType.add
-SUB = mybir.AluOpType.subtract
 RELU = mybir.ActivationFunctionType.Relu
+COPY = mybir.ActivationFunctionType.Copy
 IDENTITY = mybir.ActivationFunctionType.Identity
 TANH = mybir.ActivationFunctionType.Tanh
 
 P = 128
 PACK = 4
-CHUNK = 128
-CHUNKS = V // CHUNK
 BANK = 512
+ALIGN = 256
 
 
 def load_scale_rows(queue, plane, rows):
@@ -41,56 +39,54 @@ def tile_picked_zsgn_max_p_kernel(
         keep = ctx.enter_context(tc.tile_pool(name="keep", bufs=1))
         psum = ctx.enter_context(tc.psum_pool(name="psum", bufs=1))
 
-        offs_sb = lists.tile([P, S // 16], U16, name="offs_sb", align_bytes=256)
-        pos1_sb = lists.tile([P, V // 16], U16, name="pos1_sb", align_bytes=256)
-        pos2_sb = lists.tile([P, V // 16], U16, name="pos2_sb", align_bytes=256)
-        foe1_sb = lists.tile([P, V // 16], U16, name="foe1_sb", align_bytes=256)
-        foe2_sb = lists.tile([P, V // 16], U16, name="foe2_sb", align_bytes=256)
+        offs_sb = lists.tile([P, S // 16], U16, name="offs_sb", align_bytes=ALIGN)
+        pos1_sb = lists.tile([P, V // 16], U16, name="pos1_sb", align_bytes=ALIGN)
+        pos2_sb = lists.tile([P, V // 16], U16, name="pos2_sb", align_bytes=ALIGN)
+        foe1_sb = lists.tile([P, V // 16], U16, name="foe1_sb", align_bytes=ALIGN)
+        foe2_sb = lists.tile([P, V // 16], U16, name="foe2_sb", align_bytes=ALIGN)
 
-        x_scale_table = keep.tile([P, T], U8, name="x_scale_table", tag="scale_table", align_bytes=256)
+        x_scale_table = keep.tile([P, T], U8, name="x_scale_table", tag="scale_table", align_bytes=ALIGN)
         nc.vector.memset(x_scale_table[:].bitcast(I32), 0)
-        zero = keep.tile([P, 1], F32, name="zero", tag="foes_first", align_bytes=256)
+        zero = keep.tile([P, 1], F32, name="zero", align_bytes=ALIGN)
         nc.vector.memset(zero[:], 0.0)
-        x_sc = keep.tile([P, S], U8, name="x_sc", align_bytes=256)
+        x_sc = keep.tile([P, S], U8, name="x_sc", align_bytes=ALIGN)
         nc.vector.memset(x_sc[:].bitcast(I32), 0)
 
         w1_flat = w1.rearrange("(p j) c -> p (j c)", j=PACK)
-        w1_raw = keep.tile([P, PACK * H], F32, name="w1_raw", align_bytes=256)
+        w1_raw = keep.tile([P, PACK * H], F32, name="w1_raw", tag="w1_raw", align_bytes=ALIGN)
         nc.sync.dma_start(out=w1_raw[:, 0:H], in_=w1_flat[:, 0:H])
         nc.sync.dma_start(offs_sb[:], offs)
         nc.sync.dma_start(pos1_sb[:], pos1)
         nc.sync.dma_start(out=x_scale_table[0:P:8, :].bitcast(I32), in_=x_scales[0].bitcast(I32))
-        x_word_table = keep.tile([P, T], I32, name="x_word_table", align_bytes=256)
+        x_word_table = keep.tile([P, T], I32, name="x_word_table", align_bytes=ALIGN)
         nc.sync.dma_start(out=x_word_table[:], in_=x_words[0].rearrange("p n t -> p (n t)").bitcast(I32))
         nc.sync.dma_start(out=w1_raw[:, H:], in_=w1_flat[:, H:])
         nc.sync.dma_start(pos2_sb[:], pos2)
         nc.sync.dma_start(foe1_sb[:], foe1)
         nc.sync.dma_start(foe2_sb[:], foe2)
 
-        relu_bias = keep.tile([P, 1], F32, name="relu_bias", tag="held", align_bytes=256)
-        nc.scalar.activation(out=relu_bias[:], in_=zero[:], func=TANH)
+        cast_bias = keep.tile([P, 1], F32, name="cast_bias", tag="held", align_bytes=ALIGN)
+        nc.scalar.activation(out=cast_bias[:], in_=zero[:], func=TANH)
 
-        x_sc_spread = keep.tile([P, S], U8, name="x_sc_spread", align_bytes=256)
+        x_sc_spread = keep.tile([P, S], U8, name="x_sc_spread", align_bytes=ALIGN)
         nc.vector.tensor_copy(x_sc_spread[:], x_scale_table[:].indirect(offs_sb[:]))
         for q in range(4):
             nc.scalar.dma_start(
                 out=x_sc[32 * q : 32 * q + 4, :].bitcast(I32), in_=x_sc_spread[32 * q : 32 * q + 32 : 8, :].bitcast(I32)
             )
-        w23_codes = keep.tile([P, 2, 2 * N], U8, name="w23_codes", tag="scale_table", align_bytes=256)
-        w2_codes = w23_codes[:, 0, :]
-        w3_codes = w23_codes[:, 1, :]
-        nc.sync.dma_start(out=w2_codes.bitcast(I32), in_=w2_words[0].bitcast(I32))
-        nc.sync.dma_start(out=w3_codes.bitcast(I32), in_=w3_words[0].bitcast(I32))
+        w23_codes = keep.tile([P, 2, 2 * N], U8, name="w23_codes", tag="scale_table", align_bytes=ALIGN)
+        nc.sync.dma_start(out=w23_codes[:, 0, :].bitcast(I32), in_=w2_words[0].bitcast(I32))
+        nc.sync.dma_start(out=w23_codes[:, 1, :].bitcast(I32), in_=w3_words[0].bitcast(I32))
 
         src = w1_raw[:].rearrange("p (j m t) -> p m j t", j=PACK, t=PACK)
-        w1_bf_a = keep.tile([P, 2 * P * PACK], BF16, name="w1_bf_a", align_bytes=256)
+        w1_bf_a = keep.tile([P, 2 * P * PACK], BF16, name="w1_bf_a", align_bytes=ALIGN)
         dst_a = w1_bf_a[:].rearrange("p (t m j) -> p m j t", t=2, j=PACK)
-        w1_bf_b = keep.tile([P, 2 * P * PACK], BF16, name="w1_bf_b", align_bytes=256)
+        w1_bf_b = keep.tile([P, 2 * P * PACK], BF16, name="w1_bf_b", align_bytes=ALIGN)
         dst_b = w1_bf_b[:].rearrange("p (t m j) -> p m j t", t=2, j=PACK)
-        nc.scalar.activation(out=dst_a[:, 86:], in_=src[:, 86:, :, 0:2], func=IDENTITY, bias=relu_bias[:])
+        nc.scalar.activation(out=dst_a[:, 86:], in_=src[:, 86:, :, 0:2], func=IDENTITY, bias=cast_bias[:])
         nc.scalar.copy(out=dst_b[:, :88], in_=src[:, :88, :, 2:4])
-        w1_codes = keep.tile([P, PACK, P], U32, name="w1_codes", align_bytes=256)
-        w1_sc = keep.tile([P, PACK, P], U8, name="w1_sc", align_bytes=256)
+        w1_codes = keep.tile([P, PACK, P], U32, name="w1_codes", align_bytes=ALIGN)
+        w1_sc = keep.tile([P, PACK, P], U8, name="w1_sc", align_bytes=ALIGN)
 
         def quantise_w1(t0, t1, woven):
             nc.vector.quantize_mx(
@@ -100,12 +96,12 @@ def tile_picked_zsgn_max_p_kernel(
             )
 
         x_window = x_word_table[:].bitcast(U32)
-        x_first = keep.tile([P, 768], U32, name="x_first", align_bytes=256)
+        x_first = keep.tile([P, 768], U32, name="x_first", align_bytes=ALIGN)
         nc.vector.tensor_copy(x_first[:], x_window.indirect(offs_sb[:, 0:48]))
         nc.vector.tensor_copy(out=dst_a[:, :86], in_=src[:, :86, :, 0:2])
         nc.vector.tensor_copy(out=dst_b[:, 88:], in_=src[:, 88:, :, 2:4])
         quantise_w1(0, 1, w1_bf_a[:, : P * PACK])
-        x_rest = keep.tile([P, 256], U32, name="x_rest", tag="held", align_bytes=256)
+        x_rest = keep.tile([P, 256], U32, name="x_rest", tag="held", align_bytes=ALIGN)
         nc.vector.tensor_copy(x_rest[:], x_window.indirect(offs_sb[:, 48:64]))
         quantise_w1(1, 2, w1_bf_a[:, P * PACK :])
         quantise_w1(2, 4, w1_bf_b[:])
@@ -113,13 +109,13 @@ def tile_picked_zsgn_max_p_kernel(
         def picked(a, b):
             return x_first[:, a:b] if b <= 768 else x_rest[:, a - 768 : b - 768]
 
-        h = [keep.tile([P, S], F32, name="h%d" % t, align_bytes=256) for t in range(PACK)]
+        h = [keep.tile([P, S], F32, name="h%d" % t, align_bytes=ALIGN) for t in range(PACK)]
         bank = 0
         first_groups = [[(0, 256)], [(256, 512)], [(512, 768)], [(768, 896)], [(896, 1024)]]
         later_groups = [[(0, 512)], [(512, 768), (768, 1024)]]
         for t in range(PACK):
             for g, group in enumerate(first_groups if t == 0 else later_groups):
-                acc = psum.tile([P, BANK], F32, name="acc%d" % bank, tag="bank%d" % (bank % 5))
+                acc = psum.tile([P, BANK], F32, name="acc%d" % bank, tag="bank%d" % (bank % 8))
                 bank += 1
                 at = 0
                 for a, b in group:
@@ -137,124 +133,127 @@ def tile_picked_zsgn_max_p_kernel(
                 src_cols = acc[:, :at]
                 if t == 0 and g == 2:
                     nc.vector.tensor_scalar_max(dst_cols, src_cols, 0.0)
-                elif t == PACK - 1 and g == 1:
-                    nc.scalar.activation(out=dst_cols, in_=src_cols, func=RELU, bias=zero[:])
                 else:
                     nc.scalar.activation(out=dst_cols, in_=src_cols, func=RELU)
 
-        def fetch(dst_tile, t, list_sb, v0, v1):
-            nc.vector.tensor_copy(dst_tile[:, :, t, :], h[t][:].indirect(list_sb[:, v0 // 16 : v1 // 16]))
-
-        def weave(copy, woven, planes):
-            copy(
-                out=woven.rearrange("p (c i) t -> p c t i", i=4),
-                in_=planes.rearrange("p t (c i) -> p c t i", i=4),
-            )
-
-        def quantise(codes, scales, woven, v0, v1):
-            nc.vector.quantize_mx(
-                out=codes[:, v0:v1].bitcast(FP8X4),
-                scales=scales[:, v0:v1],
-                in_=woven[:, v0:v1, :].rearrange("p v t -> p (v t)"),
-            )
-
-        accs = {}
-
-        def product(which, codes, scales, c):
-            w_codes = w2_codes if which == 0 else w3_codes
-            for b in range(N // P):
-                if which == 0:
-                    accs[(b, c)] = psum.tile([P, BANK], F32, name="out%d_%d" % (b, c), tag="bank%d" % (2 * c + b))
-                nc.tensor.matmul_mx(
-                    out=accs[(b, c)][:, :CHUNK],
-                    lhsT=w_codes[:, 2 * P * b : 2 * P * (b + 1)].bitcast(FP4X4),
-                    lhsT_scale=w23_scales[:, which, P * b : P * (b + 1)],
-                    rhs=codes[:, c * CHUNK : (c + 1) * CHUNK].bitcast(FP8X4),
-                    rhs_scale=scales[:, c * CHUNK : (c + 1) * CHUNK],
-                    start=(which == 0),
-                    stop=(which == 1),
-                )
-
-        head = V - CHUNK
-        half = V // 2
-        zp_woven = keep.tile([P, V, PACK], BF16, name="zp_woven", align_bytes=256)
-        def larger_begin(name, first, second, tag):
-            diff = keep.tile([P, V], F32, name="diff" + name, tag=tag, align_bytes=256)
-            nc.gpsimd.tensor_tensor(diff[:], first, second, SUB)
-            return diff
-
-        def larger_end(name, diff, second, dst_plane):
-            excess = keep.tile([P, V], F32, name="excess" + name, tag="excess" + name, align_bytes=256)
-            nc.scalar.activation(out=excess[:], in_=diff[:], func=RELU)
-            nc.gpsimd.tensor_tensor(dst_plane, excess[:], second, ADD)
-
-        diff_slots = ["diff0", "excess0", "late_1", "excess1"]
-        pending = None
-        for t in range(PACK):
-            friend1 = keep.tile([P, V], F32, name="friend1_%d" % t, tag="late_%d" % t, align_bytes=256)
-            friend2 = keep.tile([P, V], F32, name="friend2_%d" % t, align_bytes=256)
-            nc.vector.tensor_copy(friend1[:], h[t][:].indirect(pos1_sb[:]))
-            nc.vector.tensor_copy(friend2[:], h[t][:].indirect(pos2_sb[:]))
-            diff = larger_begin("%d" % t, friend1[:], friend2[:], diff_slots[t])
-            if pending is not None:
-                larger_end(*pending)
-            pending = ("%d" % t, diff, friend2[:], zp_woven[:, :, t])
-            if t == 0:
-                larger_end(*pending)
-                pending = None
-        larger_end(*pending)
-        w23_scales = keep.tile([P, 2, N], U8, name="w23_scales", tag="late_0", align_bytes=256)
+        w23_scales = keep.tile([P, 2, N], U8, name="w23_scales", tag="w1_raw", align_bytes=ALIGN)
         nc.gpsimd.memset(w23_scales[:].rearrange("p a n -> p (a n)").bitcast(I32), 0)
         load_scale_rows(nc.sync, w23_scales[:, 0, :], w2_scales[0])
         load_scale_rows(nc.sync, w23_scales[:, 1, :], w3_scales[0])
 
-        last = PACK - 1
-        tail = CHUNKS - 1
-        foes1 = keep.tile([P, CHUNKS, PACK, CHUNK], BF16, name="foes1", tag="foes_first", align_bytes=256)
-        foes2 = keep.tile([P, CHUNKS, PACK, CHUNK], BF16, name="foes2", tag="late_3", align_bytes=256)
-        for t in range(PACK):
-            fetch(foes1, t, foe1_sb, 0, V)
-        for t in range(last):
-            fetch(foes2, t, foe2_sb, 0, V)
-        fetch(foes2[:, :tail], last, foe2_sb, 0, head)
-        nc.scalar.copy(out=foes2[:, tail, last, :], in_=foes1[:, tail, last, :])
-        zp_codes = keep.tile([P, V], U32, name="zp_codes", align_bytes=256)
-        zp_sc = keep.tile([P, V], U8, name="zp_sc", align_bytes=256)
-        quantise(zp_codes, zp_sc, zp_woven, 0, half)
-        for c in range(CHUNKS // 2):
-            product(0, zp_codes, zp_sc, c)
-        zn = keep.tile([P, CHUNKS + 1, PACK * CHUNK], BF16, name="zn", tag="excess3", align_bytes=256)
-        tail2 = zn[:, tail, :].rearrange("p (v t) -> p v t", t=PACK)
-        tail1 = zn[:, tail + 1, :].rearrange("p (v t) -> p v t", t=PACK)
-        weave(nc.scalar.copy, tail1, foes1[:, tail])
-        weave(nc.scalar.copy, tail2, foes2[:, tail])
-        zn_woven = keep.tile([P, head, PACK], BF16, name="zn_woven", align_bytes=256)
-        zn_codes = keep.tile([P, V], U32, name="zn_codes", align_bytes=256)
-        zn_sc = keep.tile([P, V], U8, name="zn_sc", align_bytes=256)
+        units = [(0, 0, 256), (0, 256, 512), (1, 0, 256), (1, 256, 384), (1, 384, 512)]
+        pairs = [(pos1_sb, pos2_sb), (foe1_sb, foe2_sb)]
+        chunks = [(0, 256), (256, 384), (384, 512)]
+        z_codes = keep.tile([P, 2, V], U32, name="z_codes", align_bytes=ALIGN)
+        z_sc = keep.tile([P, 2, V], U8, name="z_sc", align_bytes=ALIGN)
+        fetched, larger, woven, accs = {}, {}, {}, {}
 
-        def larger_foes(c):
-            planes = zn[:, c, :].rearrange("p (t v) -> p t v", t=PACK)
-            nc.vector.tensor_tensor(planes, foes1[:, c], foes2[:, c], MAX)
-            weave(nc.scalar.copy, zn_woven[:, c * CHUNK : (c + 1) * CHUNK, :], planes)
+        def open_unit(u):
+            width = units[u][2] - units[u][1]
+            fetched[u] = keep.tile([P, 2 * PACK * width], BF16, name="fetched%d" % u, tag="fetched%d" % (u % 2), align_bytes=ALIGN)
 
-        larger_foes(0)
-        larger_foes(1)
-        quantise(zp_codes, zp_sc, zp_woven, half, V)
-        for c in range(CHUNKS // 2, CHUNKS):
-            product(0, zp_codes, zp_sc, c)
-        larger_foes(2)
-        quantise(zn_codes, zn_sc, zn_woven, 0, CHUNK)
-        nc.vector.tensor_copy(tail1[:, :, 3], h[3][:].indirect(foe2_sb[:, head // 16 :]))
-        quantise(zn_codes, zn_sc, zn_woven, CHUNK, 2 * CHUNK)
-        nc.vector.tensor_tensor(zn[:, 1, :], zn[:, tail + 1, :], zn[:, tail, :], MAX)
-        quantise(zn_codes, zn_sc, zn_woven, 2 * CHUNK, head)
-        nc.vector.quantize_mx(out=zn_codes[:, head:].bitcast(FP8X4), scales=zn_sc[:, head:], in_=zn[:, 1, :])
+        def fetch(on_scalar, u, t, d):
+            side, v0, v1 = units[u]
+            at = (d * PACK + t) * (v1 - v0)
+            dst = fetched[u][:, at : at + v1 - v0]
+            looked_up = h[t][:].indirect(pairs[side][d][:, v0 // 16 : v1 // 16])
+            if on_scalar:
+                nc.scalar.activation(out=dst, in_=looked_up, func=COPY)
+            else:
+                nc.vector.tensor_copy(dst, looked_up)
 
-        res = keep.tile([P, N // P, V], F32, name="res", align_bytes=256)
+        def take_larger(u):
+            n = PACK * (units[u][2] - units[u][1])
+            larger[u] = keep.tile([P, n], BF16, name="larger%d" % u, align_bytes=ALIGN)
+            nc.vector.tensor_tensor(larger[u][:], fetched[u][:, :n], fetched[u][:, n:], MAX)
+
+        def weave(u):
+            n = PACK * (units[u][2] - units[u][1])
+            woven[u] = keep.tile([P, n], BF16, name="woven%d" % u, align_bytes=ALIGN)
+            nc.vector.tensor_copy(
+                out=woven[u][:].rearrange("p (c i t) -> p c t i", i=4, t=PACK),
+                in_=larger[u][:].rearrange("p (t c i) -> p c t i", i=4, t=PACK),
+            )
+
+        def quantise(u):
+            side, v0, v1 = units[u]
+            nc.vector.quantize_mx(out=z_codes[:, side, v0:v1].bitcast(FP8X4), scales=z_sc[:, side, v0:v1], in_=woven[u][:])
+            for c, (c0, c1) in enumerate(chunks):
+                if v0 <= c0 and c1 <= v1:
+                    product(side, c)
+
+        res = keep.tile([P, N // P, V], F32, name="res", align_bytes=ALIGN)
         out_v = out.rearrange("(b p) v -> p b v", p=P)
-        for c in range(CHUNKS):
-            cols = slice(c * CHUNK, (c + 1) * CHUNK)
-            product(1, zn_codes, zn_sc, c)
+
+        def product(side, c):
+            c0, c1 = chunks[c]
             for b in range(N // P):
-                nc.scalar.activation(out=res[:, b, cols], in_=accs[(b, c)][:, :CHUNK], func=TANH)
-                nc.sync.dma_start(out=out_v[:, b, cols], in_=res[:, b, cols])
+                if side == 0:
+                    accs[(b, c)] = psum.tile([P, BANK], F32, name="out%d_%d" % (b, c), tag="bank%d" % (2 * c + b))
+                nc.tensor.matmul_mx(
+                    out=accs[(b, c)][:, : c1 - c0],
+                    lhsT=w23_codes[:, side, 2 * P * b : 2 * P * (b + 1)].bitcast(FP4X4),
+                    lhsT_scale=w23_scales[:, side, P * b : P * (b + 1)],
+                    rhs=z_codes[:, side, c0:c1].bitcast(FP8X4),
+                    rhs_scale=z_sc[:, side, c0:c1],
+                    start=(side == 0),
+                    stop=(side == 1),
+                )
+
+        def finish(c):
+            c0, c1 = chunks[c]
+            for b in range(N // P):
+                nc.scalar.activation(out=res[:, b, c0:c1], in_=accs[(b, c)][:, : c1 - c0], func=TANH)
+                nc.sync.dma_start(out=out_v[:, b, c0:c1], in_=res[:, b, c0:c1])
+
+        on_v, on_s = False, True
+        open_unit(0)
+        open_unit(1)
+        for t in range(3):
+            for d in range(2):
+                fetch(on_v, 0, t, d)
+        for d in range(2):
+            fetch(on_s, 0, 3, d)
+        for d in range(2):
+            fetch(on_v, 1, 0, d)
+        for t in (2, 3):
+            for d in range(2):
+                fetch(on_s, 1, t, d)
+        take_larger(0)
+        fetch(on_v, 1, 1, 0)
+        weave(0)
+        fetch(on_v, 1, 1, 1)
+        quantise(0)
+        open_unit(2)
+        for t in range(3):
+            for d in range(2):
+                fetch(on_s, 2, t, d)
+        take_larger(1)
+        fetch(on_v, 2, 3, 0)
+        weave(1)
+        fetch(on_v, 2, 3, 1)
+        quantise(1)
+        open_unit(3)
+        for t, d in [(0, 0), (0, 1), (1, 0), (1, 1), (2, 0)]:
+            fetch(on_s, 3, t, d)
+        fetch(on_v, 3, 2, 1)
+        take_larger(2)
+        fetch(on_v, 3, 3, 0)
+        weave(2)
+        fetch(on_v, 3, 3, 1)
+        quantise(2)
+        open_unit(4)
+        for t in range(3):
+            for d in range(2):
+                fetch(on_s, 4, t, d)
+        take_larger(3)
+        fetch(on_v, 4, 3, 0)
+        weave(3)
+        fetch(on_v, 4, 3, 1)
+        quantise(3)
+        finish(0)
+        take_larger(4)
+        weave(4)
+        finish(1)
+        quantise(4)
+        finish(2)

@@ -14,6 +14,8 @@ U8 = mybir.dt.uint8
 FP8X4 = mybir.dt.float8_e4m3fn_x4
 FP4X4 = mybir.dt.float4_e2m1fn_x4
 MAX = mybir.AluOpType.max
+MULT = mybir.AluOpType.mult
+ADD = mybir.AluOpType.add
 RELU = mybir.ActivationFunctionType.Relu
 COPY = mybir.ActivationFunctionType.Copy
 IDENTITY = mybir.ActivationFunctionType.Identity
@@ -96,7 +98,7 @@ def tile_picked_zsgn_max_p_kernel(
             )
 
         x_window = x_word_table[:].bitcast(U32)
-        x_first = keep.tile([P, 768], U32, name="x_first", align_bytes=ALIGN)
+        x_first = keep.tile([P, 768], U32, name="x_first", tag="x_first", align_bytes=ALIGN)
         nc.vector.tensor_copy(x_first[:], x_window.indirect(offs_sb[:, 0:48]))
         nc.vector.tensor_copy(out=dst_a[:, :86], in_=src[:, :86, :, 0:2])
         nc.vector.tensor_copy(out=dst_b[:, 88:], in_=src[:, 88:, :, 2:4])
@@ -141,43 +143,69 @@ def tile_picked_zsgn_max_p_kernel(
         load_scale_rows(nc.sync, w23_scales[:, 0, :], w2_scales[0])
         load_scale_rows(nc.sync, w23_scales[:, 1, :], w3_scales[0])
 
-        units = [(0, 0, 256), (0, 256, 512), (1, 0, 256), (1, 256, 384), (1, 384, 512)]
         pairs = [(pos1_sb, pos2_sb), (foe1_sb, foe2_sb)]
-        chunks = [(0, 256), (256, 384), (384, 512)]
+        chunks = [(0, 128), (128, 256), (256, 384), (384, 512)]
         z_codes = keep.tile([P, 2, V], U32, name="z_codes", align_bytes=ALIGN)
         z_sc = keep.tile([P, 2, V], U8, name="z_sc", align_bytes=ALIGN)
-        fetched, larger, woven, accs = {}, {}, {}, {}
+        accs = {}
+        area_a = keep.tile([P, 5 * V], BF16, name="area_a", align_bytes=ALIGN)
+        area_b = keep.tile([P, 4 * V], BF16, name="area_b", align_bytes=ALIGN)
+        area_c = keep.tile([P, 4 * V], BF16, name="area_c", tag="x_first", align_bytes=ALIGN)
+        zp = keep.tile([P, 4 * V], BF16, name="zp", align_bytes=ALIGN)
+        z_woven = keep.tile([P, 4 * V], BF16, name="z_woven", align_bytes=ALIGN)
+        planes = {(0, 0): area_a[:, V:], (0, 1): area_b[:], (1, 0): area_a[:, : 4 * V], (1, 1): area_c[:]}
+        larger = {(0, 0, V): zp[:]}
+        woven = [z_woven[:], z_woven[:]]
 
-        def open_unit(u):
-            width = units[u][2] - units[u][1]
-            fetched[u] = keep.tile([P, 2 * PACK * width], BF16, name="fetched%d" % u, tag="fetched%d" % (u % 2), align_bytes=ALIGN)
-
-        def fetch(on_scalar, u, t, d):
-            side, v0, v1 = units[u]
-            at = (d * PACK + t) * (v1 - v0)
-            dst = fetched[u][:, at : at + v1 - v0]
+        def fetch(on_scalar, side, t, d, v0, v1):
+            dst = planes[(side, d)][:, t * V + v0 : t * V + v1]
             looked_up = h[t][:].indirect(pairs[side][d][:, v0 // 16 : v1 // 16])
             if on_scalar:
                 nc.scalar.activation(out=dst, in_=looked_up, func=COPY)
             else:
                 nc.vector.tensor_copy(dst, looked_up)
 
-        def take_larger(u):
-            n = PACK * (units[u][2] - units[u][1])
-            larger[u] = keep.tile([P, n], BF16, name="larger%d" % u, align_bytes=ALIGN)
-            nc.vector.tensor_tensor(larger[u][:], fetched[u][:, :n], fetched[u][:, n:], MAX)
+        def by_plane(flat, v0, v1):
+            return flat.rearrange("p (t v) -> p t v", t=PACK)[:, :, v0:v1]
 
-        def weave(u):
-            n = PACK * (units[u][2] - units[u][1])
-            woven[u] = keep.tile([P, n], BF16, name="woven%d" % u, align_bytes=ALIGN)
-            nc.vector.tensor_copy(
-                out=woven[u][:].rearrange("p (c i t) -> p c t i", i=4, t=PACK),
-                in_=larger[u][:].rearrange("p (t c i) -> p c t i", i=4, t=PACK),
+        def larger_part(side, v0, v1):
+            for (s, a, b), flat in larger.items():
+                if s == side and a <= v0 and v1 <= b:
+                    return by_plane(flat, v0 - a, v1 - a)
+
+        def take_larger(side, v0, v1):
+            nc.vector.tensor_tensor(
+                larger_part(side, v0, v1), by_plane(planes[(side, 0)], v0, v1), by_plane(planes[(side, 1)], v0, v1), MAX
             )
 
-        def quantise(u):
-            side, v0, v1 = units[u]
-            nc.vector.quantize_mx(out=z_codes[:, side, v0:v1].bitcast(FP8X4), scales=z_sc[:, side, v0:v1], in_=woven[u][:])
+        def take_larger_woven(side, v0, v1):
+            nc.vector.tensor_tensor(
+                woven[side][:, PACK * v0 : PACK * v1].rearrange("p (v t) -> p v t", t=PACK),
+                by_plane(planes[(side, 0)], v0, v1).rearrange("p t v -> p v t"),
+                by_plane(planes[(side, 1)], v0, v1).rearrange("p t v -> p v t"),
+                MAX,
+            )
+
+        def weave(copy, side, v0, v1):
+            copy(
+                out=woven[side][:, PACK * v0 : PACK * v1].rearrange("p (c i t) -> p c t i", i=4, t=PACK),
+                in_=larger_part(side, v0, v1).rearrange("p t (c i) -> p c t i", i=4),
+            )
+
+        def weave_on_gpsimd(side, v0, v1):
+            nc.gpsimd.tensor_scalar(
+                woven[side][:, PACK * v0 : PACK * v1].rearrange("p (v t) -> p v t", t=PACK),
+                larger_part(side, v0, v1).rearrange("p t v -> p v t"),
+                1.0,
+                0.0,
+                MULT,
+                ADD,
+            )
+
+        def quantise(side, v0, v1):
+            nc.vector.quantize_mx(
+                out=z_codes[:, side, v0:v1].bitcast(FP8X4), scales=z_sc[:, side, v0:v1], in_=woven[side][:, PACK * v0 : PACK * v1]
+            )
             for c, (c0, c1) in enumerate(chunks):
                 if v0 <= c0 and c1 <= v1:
                     product(side, c)
@@ -207,53 +235,29 @@ def tile_picked_zsgn_max_p_kernel(
                 nc.sync.dma_start(out=out_v[:, b, c0:c1], in_=res[:, b, c0:c1])
 
         on_v, on_s = False, True
-        open_unit(0)
-        open_unit(1)
-        for t in range(3):
-            for d in range(2):
-                fetch(on_v, 0, t, d)
-        for d in range(2):
-            fetch(on_s, 0, 3, d)
-        for d in range(2):
-            fetch(on_v, 1, 0, d)
-        for t in (2, 3):
-            for d in range(2):
-                fetch(on_s, 1, t, d)
-        take_larger(0)
-        fetch(on_v, 1, 1, 0)
-        weave(0)
-        fetch(on_v, 1, 1, 1)
-        quantise(0)
-        open_unit(2)
-        for t in range(3):
-            for d in range(2):
-                fetch(on_s, 2, t, d)
-        take_larger(1)
-        fetch(on_v, 2, 3, 0)
-        weave(1)
-        fetch(on_v, 2, 3, 1)
-        quantise(1)
-        open_unit(3)
-        for t, d in [(0, 0), (0, 1), (1, 0), (1, 1), (2, 0)]:
-            fetch(on_s, 3, t, d)
-        fetch(on_v, 3, 2, 1)
-        take_larger(2)
-        fetch(on_v, 3, 3, 0)
-        weave(2)
-        fetch(on_v, 3, 3, 1)
-        quantise(2)
-        open_unit(4)
-        for t in range(3):
-            for d in range(2):
-                fetch(on_s, 4, t, d)
-        take_larger(3)
-        fetch(on_v, 4, 3, 0)
-        weave(3)
-        fetch(on_v, 4, 3, 1)
-        quantise(3)
-        finish(0)
-        take_larger(4)
-        weave(4)
-        finish(1)
-        quantise(4)
-        finish(2)
+        friends, foes = 0, 1
+        for t in (0, 1):
+            for d in (0, 1):
+                fetch(on_v, friends, t, d, 0, V)
+        for d in (0, 1):
+            fetch(on_s, friends, 2, d, 0, V)
+        fetch(on_v, friends, 3, 0, 0, V)
+        fetch(on_s, friends, 3, 1, 0, V)
+        fetch(on_v, foes, 0, 0, 0, V)
+        take_larger(friends, 0, V)
+        weave_on_gpsimd(friends, 0, V)
+        for t in (1, 2):
+            fetch(on_v, foes, t, 0, 0, V)
+        for t in (0, 1, 2):
+            fetch(on_s, foes, t, 1, 0, V)
+        quantise(friends, 0, V)
+        for c0, c1 in chunks:
+            for d in (0, 1):
+                fetch(on_s, foes, 3, d, c0, c1)
+        for c, (c0, c1) in enumerate(chunks):
+            take_larger_woven(foes, c0, c1)
+            if c > 0:
+                quantise(foes, *chunks[c - 1])
+                finish(c - 1)
+        quantise(foes, *chunks[-1])
+        finish(len(chunks) - 1)

@@ -180,9 +180,9 @@ def tile_picked_zsgn_max_p_kernel(
 
         def take_larger_woven(side, v0, v1):
             nc.vector.tensor_tensor(
-                woven[side][:, PACK * v0 : PACK * v1].rearrange("p (v t) -> p v t", t=PACK),
-                by_plane(planes[(side, 0)], v0, v1).rearrange("p t v -> p v t"),
-                by_plane(planes[(side, 1)], v0, v1).rearrange("p t v -> p v t"),
+                woven[side][:, PACK * v0 : PACK * v1].rearrange("p (c i t) -> p c t i", i=4, t=PACK),
+                by_plane(planes[(side, 0)], v0, v1).rearrange("p t (c i) -> p c t i", i=4),
+                by_plane(planes[(side, 1)], v0, v1).rearrange("p t (c i) -> p c t i", i=4),
                 MAX,
             )
 

@@ -148,12 +148,12 @@ def tile_picked_zsgn_max_p_kernel(
         z_codes = keep.tile([P, 2, V], U32, name="z_codes", align_bytes=ALIGN)
         z_sc = keep.tile([P, 2, V], U8, name="z_sc", align_bytes=ALIGN)
         accs = {}
-        area_a = keep.tile([P, 5 * V], BF16, name="area_a", align_bytes=ALIGN)
+        area_a = keep.tile([P, 4 * V], BF16, name="area_a", align_bytes=ALIGN)
         area_b = keep.tile([P, 4 * V], BF16, name="area_b", align_bytes=ALIGN)
         area_c = keep.tile([P, 4 * V], BF16, name="area_c", tag="x_first", align_bytes=ALIGN)
         zp = keep.tile([P, 4 * V], BF16, name="zp", align_bytes=ALIGN)
         z_woven = keep.tile([P, 4 * V], BF16, name="z_woven", align_bytes=ALIGN)
-        planes = {(0, 0): area_a[:, V:], (0, 1): area_b[:], (1, 0): area_a[:, : 4 * V], (1, 1): area_c[:]}
+        planes = {(0, 0): area_a[:], (0, 1): area_b[:], (1, 0): area_a[:], (1, 1): area_c[:]}
         larger = {(0, 0, V): zp[:]}
         woven = [z_woven[:], z_woven[:]]
 
@@ -239,21 +239,24 @@ def tile_picked_zsgn_max_p_kernel(
         for t in (0, 1):
             for d in (0, 1):
                 fetch(on_v, friends, t, d, 0, V)
-        for d in (0, 1):
-            fetch(on_s, friends, 2, d, 0, V)
+        fetch(on_v, friends, 2, 1, 0, 256)
+        fetch(on_s, friends, 2, 0, 0, V)
+        fetch(on_s, friends, 2, 1, 256, V)
         fetch(on_v, friends, 3, 0, 0, V)
         fetch(on_s, friends, 3, 1, 0, V)
-        fetch(on_v, foes, 0, 0, 0, V)
         take_larger(friends, 0, V)
         weave_on_gpsimd(friends, 0, V)
-        for t in (1, 2):
-            fetch(on_v, foes, t, 0, 0, V)
         for t in (0, 1, 2):
             fetch(on_s, foes, t, 1, 0, V)
+        for t in (0, 1):
+            fetch(on_v, foes, t, 0, 0, V)
+        fetch(on_s, foes, 2, 0, 0, V)
+        fetch(on_v, foes, 3, 0, 0, 256)
         quantise(friends, 0, V)
         for c0, c1 in chunks:
-            for d in (0, 1):
-                fetch(on_s, foes, 3, d, c0, c1)
+            if c0 >= 256:
+                fetch(on_s, foes, 3, 0, c0, c1)
+            fetch(on_s, foes, 3, 1, c0, c1)
         for c, (c0, c1) in enumerate(chunks):
             take_larger_woven(foes, c0, c1)
             if c > 0:

@@ -192,6 +192,24 @@ def tile_picked_zsgn_max_p_kernel(
                 in_=larger_part(side, v0, v1).rearrange("p t (c i) -> p c t i", i=4),
             )
 
+        def take_larger_friends():
+            nc.vector.tensor_tensor(
+                zp[:].rearrange("p (c t i) -> p c t i", t=PACK, i=4),
+                planes[(0, 0)].rearrange("p (t c i) -> p c t i", t=PACK, i=4),
+                planes[(0, 1)].rearrange("p (t c i) -> p c t i", t=PACK, i=4),
+                MAX,
+            )
+
+        def weave_friends():
+            nc.gpsimd.tensor_scalar(
+                woven[0].rearrange("p (c i t) -> p c i t", t=PACK, i=4),
+                zp[:].rearrange("p (c t i) -> p c i t", t=PACK, i=4),
+                1.0,
+                0.0,
+                MULT,
+                ADD,
+            )
+
         def weave_on_gpsimd(side, v0, v1):
             nc.gpsimd.tensor_scalar(
                 woven[side][:, PACK * v0 : PACK * v1].rearrange("p (v t) -> p v t", t=PACK),
@@ -244,17 +262,17 @@ def tile_picked_zsgn_max_p_kernel(
         fetch(on_s, friends, 2, 1, 256, V)
         fetch(on_v, friends, 3, 0, 0, V)
         fetch(on_s, friends, 3, 1, 0, V)
-        take_larger(friends, 0, V)
-        weave_on_gpsimd(friends, 0, V)
+        take_larger_friends()
+        weave_friends()
         for t in (0, 1, 2):
             fetch(on_s, foes, t, 1, 0, V)
         for t in (0, 1):
             fetch(on_v, foes, t, 0, 0, V)
         fetch(on_s, foes, 2, 0, 0, V)
-        fetch(on_v, foes, 3, 0, 0, 256)
+        fetch(on_v, foes, 3, 0, 0, 128)
         quantise(friends, 0, V)
         for c0, c1 in chunks:
-            if c0 >= 256:
+            if c0 >= 128:
                 fetch(on_s, foes, 3, 0, c0, c1)
             fetch(on_s, foes, 3, 1, c0, c1)
         for c, (c0, c1) in enumerate(chunks):

@@ -49,7 +49,7 @@ def tile_picked_zsgn_max_p_kernel(
 
         x_scale_table = keep.tile([P, T], U8, name="x_scale_table", tag="scale_table", align_bytes=ALIGN)
         nc.vector.memset(x_scale_table[:].bitcast(I32), 0)
-        zero = keep.tile([P, 1], F32, name="zero", align_bytes=ALIGN)
+        zero = keep.tile([P, 1], F32, name="zero", tag="zp", align_bytes=ALIGN)
         nc.vector.memset(zero[:], 0.0)
         x_sc = keep.tile([P, S], U8, name="x_sc", align_bytes=ALIGN)
         nc.vector.memset(x_sc[:].bitcast(I32), 0)
@@ -135,6 +135,8 @@ def tile_picked_zsgn_max_p_kernel(
                 src_cols = acc[:, :at]
                 if t == 0 and g == 2:
                     nc.vector.tensor_scalar_max(dst_cols, src_cols, 0.0)
+                elif t == PACK - 1 and g == 1:
+                    nc.scalar.activation(out=dst_cols, in_=src_cols, func=RELU, bias=zero[:])
                 else:
                     nc.scalar.activation(out=dst_cols, in_=src_cols, func=RELU)
 
@@ -148,17 +150,17 @@ def tile_picked_zsgn_max_p_kernel(
         z_codes = keep.tile([P, 2, V], U32, name="z_codes", align_bytes=ALIGN)
         z_sc = keep.tile([P, 2, V], U8, name="z_sc", align_bytes=ALIGN)
         accs = {}
-        area_a = keep.tile([P, 4 * V], BF16, name="area_a", align_bytes=ALIGN)
-        area_b = keep.tile([P, 4 * V], BF16, name="area_b", align_bytes=ALIGN)
+        area_a = keep.tile([P, 8 * V], BF16, name="area_a", align_bytes=ALIGN)
         area_c = keep.tile([P, 4 * V], BF16, name="area_c", tag="x_first", align_bytes=ALIGN)
-        zp = keep.tile([P, 4 * V], BF16, name="zp", align_bytes=ALIGN)
+        zp = keep.tile([P, 4 * V], BF16, name="zp", tag="zp", align_bytes=ALIGN)
         z_woven = keep.tile([P, 4 * V], BF16, name="z_woven", align_bytes=ALIGN)
-        planes = {(0, 0): area_a[:], (0, 1): area_b[:], (1, 0): area_a[:], (1, 1): area_c[:]}
+        planes = {(0, 0): area_a[:, : 4 * V], (0, 1): area_a[:, 4 * V :], (1, 0): area_a[:, V : 5 * V], (1, 1): area_c[:]}
         larger = {(0, 0, V): zp[:]}
         woven = [z_woven[:], z_woven[:]]
 
         def fetch(on_scalar, side, t, d, v0, v1):
-            dst = planes[(side, d)][:, t * V + v0 : t * V + v1]
+            slot = (t + 2) % PACK if (side, d) == (0, 1) else t
+            dst = planes[(side, d)][:, slot * V + v0 : slot * V + v1]
             looked_up = h[t][:].indirect(pairs[side][d][:, v0 // 16 : v1 // 16])
             if on_scalar:
                 nc.scalar.activation(out=dst, in_=looked_up, func=COPY)
@@ -192,11 +194,11 @@ def tile_picked_zsgn_max_p_kernel(
                 in_=larger_part(side, v0, v1).rearrange("p t (c i) -> p c t i", i=4),
             )
 
-        def take_larger_friends():
+        def take_larger_friends(t0, t1):
             nc.vector.tensor_tensor(
-                zp[:].rearrange("p (c t i) -> p c t i", t=PACK, i=4),
-                planes[(0, 0)].rearrange("p (t c i) -> p c t i", t=PACK, i=4),
-                planes[(0, 1)].rearrange("p (t c i) -> p c t i", t=PACK, i=4),
+                zp[:].rearrange("p (c t i) -> p c t i", t=PACK, i=4)[:, :, t0:t1],
+                planes[(0, 0)].rearrange("p (t c i) -> p c t i", t=PACK, i=4)[:, :, t0:t1],
+                planes[(0, 1)].rearrange("p (t c i) -> p c t i", t=PACK, i=4)[:, :, 2 - t0 : 4 - t0],
                 MAX,
             )
 
@@ -257,12 +259,12 @@ def tile_picked_zsgn_max_p_kernel(
         for t in (0, 1):
             for d in (0, 1):
                 fetch(on_v, friends, t, d, 0, V)
-        fetch(on_v, friends, 2, 1, 0, 256)
+        fetch(on_v, friends, 2, 1, 0, V)
         fetch(on_s, friends, 2, 0, 0, V)
-        fetch(on_s, friends, 2, 1, 256, V)
         fetch(on_v, friends, 3, 0, 0, V)
         fetch(on_s, friends, 3, 1, 0, V)
-        take_larger_friends()
+        take_larger_friends(0, 2)
+        take_larger_friends(2, 4)
         weave_friends()
         for t in (0, 1, 2):
             fetch(on_s, foes, t, 1, 0, V)
@@ -270,7 +272,8 @@ def tile_picked_zsgn_max_p_kernel(
             fetch(on_v, foes, t, 0, 0, V)
         fetch(on_s, foes, 2, 0, 0, V)
         fetch(on_v, foes, 3, 0, 0, 128)
-        quantise(friends, 0, V)
+        quantise(friends, 0, 256)
+        quantise(friends, 256, V)
         for c0, c1 in chunks:
             if c0 >= 128:
                 fetch(on_s, foes, 3, 0, c0, c1)

@@ -259,8 +259,9 @@ def tile_picked_zsgn_max_p_kernel(
         for t in (0, 1):
             for d in (0, 1):
                 fetch(on_v, friends, t, d, 0, V)
-        fetch(on_v, friends, 2, 1, 0, V)
+        fetch(on_v, friends, 2, 1, 0, 384)
         fetch(on_s, friends, 2, 0, 0, V)
+        fetch(on_s, friends, 2, 1, 384, V)
         fetch(on_v, friends, 3, 0, 0, V)
         fetch(on_s, friends, 3, 1, 0, V)
         take_larger_friends(0, 2)

@@ -259,11 +259,11 @@ def tile_picked_zsgn_max_p_kernel(
         for t in (0, 1):
             for d in (0, 1):
                 fetch(on_v, friends, t, d, 0, V)
-        fetch(on_v, friends, 2, 1, 0, 384)
-        fetch(on_s, friends, 2, 0, 0, V)
-        fetch(on_s, friends, 2, 1, 384, V)
+        for d in (0, 1):
+            fetch(on_s, friends, 2, d, 0, V)
         fetch(on_v, friends, 3, 0, 0, V)
-        fetch(on_s, friends, 3, 1, 0, V)
+        fetch(on_v, friends, 3, 1, 0, 384)
+        fetch(on_s, friends, 3, 1, 384, V)
         take_larger_friends(0, 2)
         take_larger_friends(2, 4)
         weave_friends()

@@ -145,98 +145,56 @@ def tile_picked_zsgn_max_p_kernel(
         load_scale_rows(nc.sync, w23_scales[:, 0, :], w2_scales[0])
         load_scale_rows(nc.sync, w23_scales[:, 1, :], w3_scales[0])
 
+        friends, foes = 0, 1
+        on_vector, on_scalar = False, True
         pairs = [(pos1_sb, pos2_sb), (foe1_sb, foe2_sb)]
         chunks = [(0, 128), (128, 256), (256, 384), (384, 512)]
         z_codes = keep.tile([P, 2, V], U32, name="z_codes", align_bytes=ALIGN)
         z_sc = keep.tile([P, 2, V], U8, name="z_sc", align_bytes=ALIGN)
+        area = keep.tile([P, 2 * PACK * V], BF16, name="area", align_bytes=ALIGN)
+        second_foes = keep.tile([P, PACK * V], BF16, name="second_foes", tag="x_first", align_bytes=ALIGN)[:]
+        zp = keep.tile([P, PACK * V], BF16, name="zp", tag="zp", align_bytes=ALIGN)[:]
+        friend_planes = [area[:, : PACK * V], area[:, PACK * V :]]
+        foe_pairs = [run.rearrange("p (u v e) -> p u v e", u=2, e=2) for run in (area[:, : PACK * V], second_foes)]
+        z_woven = keep.tile([P, PACK * V], BF16, name="z_woven", align_bytes=ALIGN)
+        res = keep.tile([P, N // P, V], F32, name="res", align_bytes=ALIGN)
+        out_v = out.rearrange("(b p) v -> p b v", p=P)
         accs = {}
-        area_a = keep.tile([P, 8 * V], BF16, name="area_a", align_bytes=ALIGN)
-        area_c = keep.tile([P, 4 * V], BF16, name="area_c", tag="x_first", align_bytes=ALIGN)
-        zp = keep.tile([P, 4 * V], BF16, name="zp", tag="zp", align_bytes=ALIGN)
-        z_woven = keep.tile([P, 4 * V], BF16, name="z_woven", align_bytes=ALIGN)
-        planes = {(0, 0): area_a[:, : 4 * V], (0, 1): area_a[:, 4 * V :], (1, 0): area_a[:, V : 5 * V], (1, 1): area_c[:]}
-        larger = {(0, 0, V): zp[:]}
-        woven = [z_woven[:], z_woven[:]]
 
-        def fetch(on_scalar, side, t, d, v0, v1):
-            slot = (t + 2) % PACK if (side, d) == (0, 1) else t
-            dst = planes[(side, d)][:, slot * V + v0 : slot * V + v1]
+        def fetch(engine, side, t, d, v0, v1):
+            if side == friends:
+                dst = friend_planes[d][:, t * V + v0 : t * V + v1]
+            else:
+                dst = foe_pairs[d][:, t // 2, v0:v1, t % 2]
             looked_up = h[t][:].indirect(pairs[side][d][:, v0 // 16 : v1 // 16])
-            if on_scalar:
+            if engine == on_scalar:
                 nc.scalar.activation(out=dst, in_=looked_up, func=COPY)
             else:
                 nc.vector.tensor_copy(dst, looked_up)
 
-        def by_plane(flat, v0, v1):
-            return flat.rearrange("p (t v) -> p t v", t=PACK)[:, :, v0:v1]
-
-        def larger_part(side, v0, v1):
-            for (s, a, b), flat in larger.items():
-                if s == side and a <= v0 and v1 <= b:
-                    return by_plane(flat, v0 - a, v1 - a)
-
-        def take_larger(side, v0, v1):
-            nc.vector.tensor_tensor(
-                larger_part(side, v0, v1), by_plane(planes[(side, 0)], v0, v1), by_plane(planes[(side, 1)], v0, v1), MAX
-            )
-
-        def take_larger_woven(side, v0, v1):
-            nc.vector.tensor_tensor(
-                woven[side][:, PACK * v0 : PACK * v1].rearrange("p (c i t) -> p c t i", i=4, t=PACK),
-                by_plane(planes[(side, 0)], v0, v1).rearrange("p t (c i) -> p c t i", i=4),
-                by_plane(planes[(side, 1)], v0, v1).rearrange("p t (c i) -> p c t i", i=4),
-                MAX,
-            )
-
-        def weave(copy, side, v0, v1):
-            copy(
-                out=woven[side][:, PACK * v0 : PACK * v1].rearrange("p (c i t) -> p c t i", i=4, t=PACK),
-                in_=larger_part(side, v0, v1).rearrange("p t (c i) -> p c t i", i=4),
-            )
-
-        def take_larger_friends(t0, t1):
-            nc.vector.tensor_tensor(
-                zp[:].rearrange("p (c t i) -> p c t i", t=PACK, i=4)[:, :, t0:t1],
-                planes[(0, 0)].rearrange("p (t c i) -> p c t i", t=PACK, i=4)[:, :, t0:t1],
-                planes[(0, 1)].rearrange("p (t c i) -> p c t i", t=PACK, i=4)[:, :, 2 - t0 : 4 - t0],
-                MAX,
-            )
+        def larger_friends(t0, t1, v0, v1):
+            first, second = [planes.rearrange("p (t c i) -> p c t i", t=PACK, i=4)[:, v0 // 4 : v1 // 4, t0:t1] for planes in friend_planes]
+            nc.vector.tensor_tensor(zp.rearrange("p (c t i) -> p c t i", t=PACK, i=4)[:, v0 // 4 : v1 // 4, t0:t1], first, second, MAX)
 
         def weave_friends():
             nc.gpsimd.tensor_scalar(
-                woven[0].rearrange("p (c i t) -> p c i t", t=PACK, i=4),
-                zp[:].rearrange("p (c t i) -> p c i t", t=PACK, i=4),
+                z_woven[:].rearrange("p (c i t) -> p c i t", t=PACK, i=4),
+                zp.rearrange("p (c t i) -> p c i t", t=PACK, i=4),
                 1.0,
                 0.0,
                 MULT,
                 ADD,
             )
 
-        def weave_on_gpsimd(side, v0, v1):
-            nc.gpsimd.tensor_scalar(
-                woven[side][:, PACK * v0 : PACK * v1].rearrange("p (v t) -> p v t", t=PACK),
-                larger_part(side, v0, v1).rearrange("p t v -> p v t"),
-                1.0,
-                0.0,
-                MULT,
-                ADD,
-            )
-
-        def quantise(side, v0, v1):
-            nc.vector.quantize_mx(
-                out=z_codes[:, side, v0:v1].bitcast(FP8X4), scales=z_sc[:, side, v0:v1], in_=woven[side][:, PACK * v0 : PACK * v1]
-            )
-            for c, (c0, c1) in enumerate(chunks):
-                if v0 <= c0 and c1 <= v1:
-                    product(side, c)
-
-        res = keep.tile([P, N // P, V], F32, name="res", align_bytes=ALIGN)
-        out_v = out.rearrange("(b p) v -> p b v", p=P)
+        def larger_foes(v0, v1):
+            first, second = [foe_pairs[d][:, :, v0:v1, :].rearrange("p u v e -> p v u e") for d in (0, 1)]
+            woven = z_woven[:, PACK * v0 : PACK * v1].rearrange("p (v u e) -> p v u e", u=2, e=2)
+            nc.vector.tensor_tensor(woven, first, second, MAX)
 
         def product(side, c):
             c0, c1 = chunks[c]
             for b in range(N // P):
-                if side == 0:
+                if side == friends:
                     accs[(b, c)] = psum.tile([P, BANK], F32, name="out%d_%d" % (b, c), tag="bank%d" % (2 * c + b))
                 nc.tensor.matmul_mx(
                     out=accs[(b, c)][:, : c1 - c0],
@@ -244,9 +202,17 @@ def tile_picked_zsgn_max_p_kernel(
                     lhsT_scale=w23_scales[:, side, P * b : P * (b + 1)],
                     rhs=z_codes[:, side, c0:c1].bitcast(FP8X4),
                     rhs_scale=z_sc[:, side, c0:c1],
-                    start=(side == 0),
-                    stop=(side == 1),
+                    start=(side == friends),
+                    stop=(side == foes),
                 )
+
+        def quantise(side, v0, v1):
+            nc.vector.quantize_mx(
+                out=z_codes[:, side, v0:v1].bitcast(FP8X4), scales=z_sc[:, side, v0:v1], in_=z_woven[:, PACK * v0 : PACK * v1]
+            )
+            for c, (c0, c1) in enumerate(chunks):
+                if v0 <= c0 and c1 <= v1:
+                    product(side, c)
 
         def finish(c):
             c0, c1 = chunks[c]
@@ -254,33 +220,34 @@ def tile_picked_zsgn_max_p_kernel(
                 nc.scalar.activation(out=res[:, b, c0:c1], in_=accs[(b, c)][:, : c1 - c0], func=TANH)
                 nc.sync.dma_start(out=out_v[:, b, c0:c1], in_=res[:, b, c0:c1])
 
-        on_v, on_s = False, True
-        friends, foes = 0, 1
+        FRIENDS_SHARE = 384
+        FOES_SHARE = 160
+        HALF = V // 2
         for t in (0, 1):
             for d in (0, 1):
-                fetch(on_v, friends, t, d, 0, V)
+                fetch(on_vector, friends, t, d, 0, V)
         for d in (0, 1):
-            fetch(on_s, friends, 2, d, 0, V)
-        fetch(on_v, friends, 3, 0, 0, V)
-        fetch(on_v, friends, 3, 1, 0, 384)
-        fetch(on_s, friends, 3, 1, 384, V)
-        take_larger_friends(0, 2)
-        take_larger_friends(2, 4)
+            fetch(on_scalar, friends, 2, d, 0, V)
+        fetch(on_vector, friends, 3, 0, 0, V)
+        fetch(on_vector, friends, 3, 1, 0, FRIENDS_SHARE)
+        fetch(on_scalar, friends, 3, 1, FRIENDS_SHARE, V)
+        larger_friends(0, 2, 0, V)
+        larger_friends(2, 4, 0, V)
         weave_friends()
-        for t in (0, 1, 2):
-            fetch(on_s, foes, t, 1, 0, V)
         for t in (0, 1):
-            fetch(on_v, foes, t, 0, 0, V)
-        fetch(on_s, foes, 2, 0, 0, V)
-        fetch(on_v, foes, 3, 0, 0, 128)
-        quantise(friends, 0, 256)
-        quantise(friends, 256, V)
+            fetch(on_vector, foes, t, 0, 0, V)
+            fetch(on_vector, foes, t + 2, 0, 0, FOES_SHARE)
+        for t in (0, 2, 1):
+            fetch(on_scalar, foes, t, 1, 0, V)
+        fetch(on_scalar, foes, 2, 0, FOES_SHARE, V)
+        quantise(friends, 0, HALF)
+        quantise(friends, HALF, V)
         for c0, c1 in chunks:
-            if c0 >= 128:
-                fetch(on_s, foes, 3, 0, c0, c1)
-            fetch(on_s, foes, 3, 1, c0, c1)
+            if c1 > FOES_SHARE:
+                fetch(on_scalar, foes, 3, 0, max(c0, FOES_SHARE), c1)
+            fetch(on_scalar, foes, 3, 1, c0, c1)
         for c, (c0, c1) in enumerate(chunks):
-            take_larger_woven(foes, c0, c1)
+            larger_foes(c0, c1)
             if c > 0:
                 quantise(foes, *chunks[c - 1])
                 finish(c - 1)

@@ -55,7 +55,7 @@ def tile_picked_zsgn_max_p_kernel(
         nc.vector.memset(x_sc[:].bitcast(I32), 0)
 
         w1_flat = w1.rearrange("(p j) c -> p (j c)", j=PACK)
-        w1_raw = keep.tile([P, PACK * H], F32, name="w1_raw", tag="w1_raw", align_bytes=ALIGN)
+        w1_raw = keep.tile([P, PACK * H], F32, name="w1_raw", align_bytes=ALIGN)
         nc.sync.dma_start(out=w1_raw[:, 0:H], in_=w1_flat[:, 0:H])
         nc.sync.dma_start(offs_sb[:], offs)
         nc.sync.dma_start(pos1_sb[:], pos1)
@@ -83,7 +83,7 @@ def tile_picked_zsgn_max_p_kernel(
         src = w1_raw[:].rearrange("p (j m t) -> p m j t", j=PACK, t=PACK)
         w1_bf_a = keep.tile([P, 2 * P * PACK], BF16, name="w1_bf_a", align_bytes=ALIGN)
         dst_a = w1_bf_a[:].rearrange("p (t m j) -> p m j t", t=2, j=PACK)
-        w1_bf_b = keep.tile([P, 2 * P * PACK], BF16, name="w1_bf_b", align_bytes=ALIGN)
+        w1_bf_b = keep.tile([P, 2 * P * PACK], BF16, name="w1_bf_b", tag="w1_bf_b", align_bytes=ALIGN)
         dst_b = w1_bf_b[:].rearrange("p (t m j) -> p m j t", t=2, j=PACK)
         nc.scalar.activation(out=dst_a[:, 86:], in_=src[:, 86:, :, 0:2], func=IDENTITY, bias=cast_bias[:])
         nc.scalar.copy(out=dst_b[:, :88], in_=src[:, :88, :, 2:4])
@@ -140,7 +140,7 @@ def tile_picked_zsgn_max_p_kernel(
                 else:
                     nc.scalar.activation(out=dst_cols, in_=src_cols, func=RELU)
 
-        w23_scales = keep.tile([P, 2, N], U8, name="w23_scales", tag="w1_raw", align_bytes=ALIGN)
+        w23_scales = keep.tile([P, 2, N], U8, name="w23_scales", tag="w1_bf_b", align_bytes=ALIGN)
         nc.gpsimd.memset(w23_scales[:].rearrange("p a n -> p (a n)").bitcast(I32), 0)
         load_scale_rows(nc.sync, w23_scales[:, 0, :], w2_scales[0])
         load_scale_rows(nc.sync, w23_scales[:, 1, :], w3_scales[0])
@@ -220,8 +220,8 @@ def tile_picked_zsgn_max_p_kernel(
                 nc.scalar.activation(out=res[:, b, c0:c1], in_=accs[(b, c)][:, : c1 - c0], func=TANH)
                 nc.sync.dma_start(out=out_v[:, b, c0:c1], in_=res[:, b, c0:c1])
 
-        FRIENDS_SHARE = 384
-        FOES_SHARE = 160
+        FRIENDS_SHARE = 352
+        FOES_SHARE = 192
         HALF = V // 2
         for t in (0, 1):
             for d in (0, 1):

from contextlib import ExitStack

import concourse.mybir as mybir

K, T, S, V, H, N = 512, 2048, 1024, 512, 512, 256
FLOPS = 2 * K * H * S + 2 * 2 * H * N * V

F32 = mybir.dt.float32
BF16 = mybir.dt.bfloat16
I32 = mybir.dt.int32
U32 = mybir.dt.uint32
U16 = mybir.dt.uint16
U8 = mybir.dt.uint8
FP8X4 = mybir.dt.float8_e4m3fn_x4
FP4X4 = mybir.dt.float4_e2m1fn_x4
MAX = mybir.AluOpType.max
MULT = mybir.AluOpType.mult
ADD = mybir.AluOpType.add
RELU = mybir.ActivationFunctionType.Relu
COPY = mybir.ActivationFunctionType.Copy
IDENTITY = mybir.ActivationFunctionType.Identity
TANH = mybir.ActivationFunctionType.Tanh

P = 128
PACK = 4
BANK = 512
ALIGN = 256


def load_scale_rows(queue, plane, rows):
    for q in range(4):
        queue.dma_start(out=plane[32 * q : 32 * q + 4, :].bitcast(I32), in_=rows[4 * q : 4 * q + 4, :].bitcast(I32))


def tile_picked_zsgn_max_p_kernel(
    tc, x_words, x_scales, w1, w2_words, w2_scales, w3_words, w3_scales, offs, pos1, pos2, foe1, foe2, out
):
    nc = tc.nc
    with ExitStack() as ctx:
        lists = ctx.enter_context(tc.tile_pool(name="lists", bufs=1))
        keep = ctx.enter_context(tc.tile_pool(name="keep", bufs=1))
        psum = ctx.enter_context(tc.psum_pool(name="psum", bufs=1))

        offs_sb = lists.tile([P, S // 16], U16, name="offs_sb", align_bytes=ALIGN)
        pos1_sb = lists.tile([P, V // 16], U16, name="pos1_sb", align_bytes=ALIGN)
        pos2_sb = lists.tile([P, V // 16], U16, name="pos2_sb", align_bytes=ALIGN)
        foe1_sb = lists.tile([P, V // 16], U16, name="foe1_sb", align_bytes=ALIGN)
        foe2_sb = lists.tile([P, V // 16], U16, name="foe2_sb", align_bytes=ALIGN)

        x_scale_table = keep.tile([P, T], U8, name="x_scale_table", tag="scale_table", align_bytes=ALIGN)
        nc.vector.memset(x_scale_table[:].bitcast(I32), 0)
        zero = keep.tile([P, 1], F32, name="zero", tag="zp", align_bytes=ALIGN)
        nc.vector.memset(zero[:], 0.0)
        x_sc = keep.tile([P, S], U8, name="x_sc", align_bytes=ALIGN)
        nc.vector.memset(x_sc[:].bitcast(I32), 0)

        w1_flat = w1.rearrange("(p j) c -> p (j c)", j=PACK)
        w1_raw = keep.tile([P, PACK * H], F32, name="w1_raw", align_bytes=ALIGN)
        nc.sync.dma_start(out=w1_raw[:, 0:H], in_=w1_flat[:, 0:H])
        nc.sync.dma_start(offs_sb[:], offs)
        nc.sync.dma_start(pos1_sb[:], pos1)
        nc.sync.dma_start(out=x_scale_table[0:P:8, :].bitcast(I32), in_=x_scales[0].bitcast(I32))
        x_word_table = keep.tile([P, T], I32, name="x_word_table", align_bytes=ALIGN)
        nc.sync.dma_start(out=x_word_table[:], in_=x_words[0].rearrange("p n t -> p (n t)").bitcast(I32))
        nc.sync.dma_start(out=w1_raw[:, H:], in_=w1_flat[:, H:])
        nc.sync.dma_start(pos2_sb[:], pos2)
        nc.sync.dma_start(foe1_sb[:], foe1)
        nc.sync.dma_start(foe2_sb[:], foe2)

        cast_bias = keep.tile([P, 1], F32, name="cast_bias", tag="held", align_bytes=ALIGN)
        nc.scalar.activation(out=cast_bias[:], in_=zero[:], func=TANH)

        x_sc_spread = keep.tile([P, S], U8, name="x_sc_spread", align_bytes=ALIGN)
        nc.vector.tensor_copy(x_sc_spread[:], x_scale_table[:].indirect(offs_sb[:]))
        for q in range(4):
            nc.scalar.dma_start(
                out=x_sc[32 * q : 32 * q + 4, :].bitcast(I32), in_=x_sc_spread[32 * q : 32 * q + 32 : 8, :].bitcast(I32)
            )
        w23_codes = keep.tile([P, 2, 2 * N], U8, name="w23_codes", tag="scale_table", align_bytes=ALIGN)
        nc.sync.dma_start(out=w23_codes[:, 0, :].bitcast(I32), in_=w2_words[0].bitcast(I32))
        nc.sync.dma_start(out=w23_codes[:, 1, :].bitcast(I32), in_=w3_words[0].bitcast(I32))

        src = w1_raw[:].rearrange("p (j m t) -> p m j t", j=PACK, t=PACK)
        w1_bf_a = keep.tile([P, 2 * P * PACK], BF16, name="w1_bf_a", align_bytes=ALIGN)
        dst_a = w1_bf_a[:].rearrange("p (t m j) -> p m j t", t=2, j=PACK)
        w1_bf_b = keep.tile([P, 2 * P * PACK], BF16, name="w1_bf_b", tag="w1_bf_b", align_bytes=ALIGN)
        dst_b = w1_bf_b[:].rearrange("p (t m j) -> p m j t", t=2, j=PACK)
        nc.scalar.activation(out=dst_a[:, 86:], in_=src[:, 86:, :, 0:2], func=IDENTITY, bias=cast_bias[:])
        nc.scalar.copy(out=dst_b[:, :88], in_=src[:, :88, :, 2:4])
        w1_codes = keep.tile([P, PACK, P], U32, name="w1_codes", align_bytes=ALIGN)
        w1_sc = keep.tile([P, PACK, P], U8, name="w1_sc", align_bytes=ALIGN)

        def quantise_w1(t0, t1, woven):
            nc.vector.quantize_mx(
                out=w1_codes[:, t0:t1, :].rearrange("p t m -> p (t m)").bitcast(FP8X4),
                scales=w1_sc[:, t0:t1, :].rearrange("p t m -> p (t m)"),
                in_=woven,
            )

        x_window = x_word_table[:].bitcast(U32)
        x_first = keep.tile([P, 768], U32, name="x_first", tag="x_first", align_bytes=ALIGN)
        nc.vector.tensor_copy(x_first[:], x_window.indirect(offs_sb[:, 0:48]))
        nc.vector.tensor_copy(out=dst_a[:, :86], in_=src[:, :86, :, 0:2])
        nc.vector.tensor_copy(out=dst_b[:, 88:], in_=src[:, 88:, :, 2:4])
        quantise_w1(0, 1, w1_bf_a[:, : P * PACK])
        x_rest = keep.tile([P, 256], U32, name="x_rest", tag="held", align_bytes=ALIGN)
        nc.vector.tensor_copy(x_rest[:], x_window.indirect(offs_sb[:, 48:64]))
        quantise_w1(1, 2, w1_bf_a[:, P * PACK :])
        quantise_w1(2, 4, w1_bf_b[:])

        def picked(a, b):
            return x_first[:, a:b] if b <= 768 else x_rest[:, a - 768 : b - 768]

        h = [keep.tile([P, S], F32, name="h%d" % t, align_bytes=ALIGN) for t in range(PACK)]
        bank = 0
        first_groups = [[(0, 256)], [(256, 512)], [(512, 768)], [(768, 896)], [(896, 1024)]]
        later_groups = [[(0, 512)], [(512, 768), (768, 1024)]]
        for t in range(PACK):
            for g, group in enumerate(first_groups if t == 0 else later_groups):
                acc = psum.tile([P, BANK], F32, name="acc%d" % bank, tag="bank%d" % (bank % 8))
                bank += 1
                at = 0
                for a, b in group:
                    nc.tensor.matmul_mx(
                        out=acc[:, at : at + b - a],
                        lhsT=w1_codes[:, t, :].bitcast(FP8X4),
                        lhsT_scale=w1_sc[:, t, :],
                        rhs=picked(a, b).bitcast(FP8X4),
                        rhs_scale=x_sc[:, a:b],
                        start=True,
                        stop=True,
                    )
                    at += b - a
                dst_cols = h[t][:, group[0][0] : group[-1][1]]
                src_cols = acc[:, :at]
                if t == 0 and g == 2:
                    nc.vector.tensor_scalar_max(dst_cols, src_cols, 0.0)
                elif t == PACK - 1 and g == 1:
                    nc.scalar.activation(out=dst_cols, in_=src_cols, func=RELU, bias=zero[:])
                else:
                    nc.scalar.activation(out=dst_cols, in_=src_cols, func=RELU)

        w23_scales = keep.tile([P, 2, N], U8, name="w23_scales", tag="w1_bf_b", align_bytes=ALIGN)
        nc.gpsimd.memset(w23_scales[:].rearrange("p a n -> p (a n)").bitcast(I32), 0)
        load_scale_rows(nc.sync, w23_scales[:, 0, :], w2_scales[0])
        load_scale_rows(nc.sync, w23_scales[:, 1, :], w3_scales[0])

        friends, foes = 0, 1
        on_vector, on_scalar = False, True
        pairs = [(pos1_sb, pos2_sb), (foe1_sb, foe2_sb)]
        chunks = [(0, 128), (128, 256), (256, 384), (384, 512)]
        z_codes = keep.tile([P, 2, V], U32, name="z_codes", align_bytes=ALIGN)
        z_sc = keep.tile([P, 2, V], U8, name="z_sc", align_bytes=ALIGN)
        area = keep.tile([P, 2 * PACK * V], BF16, name="area", align_bytes=ALIGN)
        second_foes = keep.tile([P, PACK * V], BF16, name="second_foes", tag="x_first", align_bytes=ALIGN)[:]
        zp = keep.tile([P, PACK * V], BF16, name="zp", tag="zp", align_bytes=ALIGN)[:]
        friend_planes = [area[:, : PACK * V], area[:, PACK * V :]]
        foe_pairs = [run.rearrange("p (u v e) -> p u v e", u=2, e=2) for run in (area[:, : PACK * V], second_foes)]
        z_woven = keep.tile([P, PACK * V], BF16, name="z_woven", align_bytes=ALIGN)
        res = keep.tile([P, N // P, V], F32, name="res", align_bytes=ALIGN)
        out_v = out.rearrange("(b p) v -> p b v", p=P)
        accs = {}

        def fetch(engine, side, t, d, v0, v1):
            if side == friends:
                dst = friend_planes[d][:, t * V + v0 : t * V + v1]
            else:
                dst = foe_pairs[d][:, t // 2, v0:v1, t % 2]
            looked_up = h[t][:].indirect(pairs[side][d][:, v0 // 16 : v1 // 16])
            if engine == on_scalar:
                nc.scalar.activation(out=dst, in_=looked_up, func=COPY)
            else:
                nc.vector.tensor_copy(dst, looked_up)

        def larger_friends(t0, t1, v0, v1):
            first, second = [planes.rearrange("p (t c i) -> p c t i", t=PACK, i=4)[:, v0 // 4 : v1 // 4, t0:t1] for planes in friend_planes]
            nc.vector.tensor_tensor(zp.rearrange("p (c t i) -> p c t i", t=PACK, i=4)[:, v0 // 4 : v1 // 4, t0:t1], first, second, MAX)

        def weave_friends():
            nc.gpsimd.tensor_scalar(
                z_woven[:].rearrange("p (c i t) -> p c i t", t=PACK, i=4),
                zp.rearrange("p (c t i) -> p c i t", t=PACK, i=4),
                1.0,
                0.0,
                MULT,
                ADD,
            )

        def larger_foes(v0, v1):
            first, second = [foe_pairs[d][:, :, v0:v1, :].rearrange("p u v e -> p v u e") for d in (0, 1)]
            woven = z_woven[:, PACK * v0 : PACK * v1].rearrange("p (v u e) -> p v u e", u=2, e=2)
            nc.vector.tensor_tensor(woven, first, second, MAX)

        def product(side, c):
            c0, c1 = chunks[c]
            for b in range(N // P):
                if side == friends:
                    accs[(b, c)] = psum.tile([P, BANK], F32, name="out%d_%d" % (b, c), tag="bank%d" % (2 * c + b))
                nc.tensor.matmul_mx(
                    out=accs[(b, c)][:, : c1 - c0],
                    lhsT=w23_codes[:, side, 2 * P * b : 2 * P * (b + 1)].bitcast(FP4X4),
                    lhsT_scale=w23_scales[:, side, P * b : P * (b + 1)],
                    rhs=z_codes[:, side, c0:c1].bitcast(FP8X4),
                    rhs_scale=z_sc[:, side, c0:c1],
                    start=(side == friends),
                    stop=(side == foes),
                )

        def quantise(side, v0, v1):
            nc.vector.quantize_mx(
                out=z_codes[:, side, v0:v1].bitcast(FP8X4), scales=z_sc[:, side, v0:v1], in_=z_woven[:, PACK * v0 : PACK * v1]
            )
            for c, (c0, c1) in enumerate(chunks):
                if v0 <= c0 and c1 <= v1:
                    product(side, c)

        def finish(c):
            c0, c1 = chunks[c]
            for b in range(N // P):
                nc.scalar.activation(out=res[:, b, c0:c1], in_=accs[(b, c)][:, : c1 - c0], func=TANH)
                nc.sync.dma_start(out=out_v[:, b, c0:c1], in_=res[:, b, c0:c1])

        FRIENDS_SHARE = 352
        FOES_SHARE = 192
        HALF = V // 2
        for t in (0, 1):
            for d in (0, 1):
                fetch(on_vector, friends, t, d, 0, V)
        for d in (0, 1):
            fetch(on_scalar, friends, 2, d, 0, V)
        fetch(on_vector, friends, 3, 0, 0, V)
        fetch(on_vector, friends, 3, 1, 0, FRIENDS_SHARE)
        fetch(on_scalar, friends, 3, 1, FRIENDS_SHARE, V)
        larger_friends(0, 2, 0, V)
        larger_friends(2, 4, 0, V)
        weave_friends()
        for t in (0, 1):
            fetch(on_vector, foes, t, 0, 0, V)
            fetch(on_vector, foes, t + 2, 0, 0, FOES_SHARE)
        for t in (0, 2, 1):
            fetch(on_scalar, foes, t, 1, 0, V)
        fetch(on_scalar, foes, 2, 0, FOES_SHARE, V)
        quantise(friends, 0, HALF)
        quantise(friends, HALF, V)
        for c0, c1 in chunks:
            if c1 > FOES_SHARE:
                fetch(on_scalar, foes, 3, 0, max(c0, FOES_SHARE), c1)
            fetch(on_scalar, foes, 3, 1, c0, c1)
        for c, (c0, c1) in enumerate(chunks):
            larger_foes(c0, c1)
            if c > 0:
                quantise(foes, *chunks[c - 1])
                finish(c - 1)
        quantise(foes, *chunks[-1])
        finish(len(chunks) - 1)
